import numpy as np
import ml_dtypes


def mxq(x, axis, fmt="e4m3"):
    dtype, down = {"e4m3": (ml_dtypes.float8_e4m3fn, 7), "e5m2": (ml_dtypes.float8_e5m2, 14)}[fmt]
    v = np.moveaxis(np.asarray(x, np.float32).astype(ml_dtypes.bfloat16).astype(np.float64), axis, -1)
    blocks = v.reshape(v.shape[:-1] + (-1, 32))
    amax = np.abs(blocks).max(-1, keepdims=True)
    byte = np.maximum(np.where(amax > 0, np.frexp(amax)[1] - 1 + 127, 0) - down, 1)
    scale = np.exp2(byte - 127.0)
    codes = (blocks / scale).astype(np.float32).astype(dtype).astype(np.float64)
    return np.moveaxis((codes * scale).reshape(v.shape), -1, axis)


WIDE = False


def mx_kscale(k):
    if not WIDE:
        return np.ones(k)
    levels = np.array([10, -10, 5, -5, 0])
    if k % 512:
        return np.exp2(np.random.permutation(np.resize(levels, k // 32))).repeat(32)
    a = np.empty((k // 512, 16))
    for p in range(k // 512):
        a[p, :8] = np.random.permutation(np.resize(levels, 8))
        for g in range(8):
            far = levels[np.abs(levels - a[p, g]) >= 10]
            a[p, g + 8] = far[np.random.randint(len(far))]
    return np.exp2(a.ravel()).repeat(32)


BF16 = ml_dtypes.bfloat16


def bf(x):
    return np.asarray(x, np.float32).astype(BF16)


def f64(x):
    return np.asarray(x).astype(np.float64)


E2M1 = np.array([0.0, 0.5, 1.0, 1.5, 2.0, 3.0, 4.0, 6.0, -0.0, -0.5, -1.0, -1.5, -2.0, -3.0, -4.0, -6.0])


def pack_weight(w, fmt):
    k, n = w.shape
    w = f64(bf(w)).reshape(k // 32, 32, n)
    amax = np.abs(w).max(1)
    if fmt == "e4m3":
        byte = np.frexp(amax)[1] - 1 + 127 - 7
    else:
        mant, ex = np.frexp(amax / 6.0)
        byte = np.where(mant > 0.5, ex, ex - 1) + 127
    byte = np.clip(np.where(amax > 0, byte, 1), 1, 254)
    scaled = (w * np.exp2(127.0 - byte)[:, None, :]).reshape(k, n).astype(np.float32)
    by_word = np.ascontiguousarray(scaled.reshape(k // 512, 128, 4, n).transpose(0, 1, 3, 2))
    if fmt == "e4m3":
        words = by_word.astype(ml_dtypes.float8_e4m3fn).view(np.uint8)
    else:
        c = by_word.astype(ml_dtypes.float4_e2m1fn).view(np.uint8) & 0xF
        words = c[..., 0::2] | (c[..., 1::2] << 4)
    return np.ascontiguousarray(words), np.ascontiguousarray(byte.astype(np.uint8).reshape(k // 512, 16, n))


def unpack_weight(words, scales, fmt):
    g, p, n, _ = words.shape
    if fmt == "e4m3":
        vals = np.ascontiguousarray(words).view(ml_dtypes.float8_e4m3fn).astype(np.float64)
    else:
        nib = np.empty((g, p, n, 4), np.uint8)
        nib[..., 0::2] = words & 0xF
        nib[..., 1::2] = words >> 4
        vals = E2M1[nib]
    vals = vals * np.repeat(np.exp2(scales.astype(np.float64) - 127.0), 8, axis=1)[..., None]
    return vals.transpose(0, 1, 3, 2).reshape(g * 512, n)
def pack4(w):
    words, scales = pack_weight(w, "e2m1")
    return words.reshape(words.shape[0], 128, -1), scales


def unpack4(words, scales):
    return unpack_weight(words.reshape(words.shape[0], 128, -1, 2), scales, "e2m1")


def planes(Y):
    n, m = Y.shape
    b = f64(bf(Y)).reshape(n // 32, 32, m)
    amax = np.abs(b).max(1)
    byte = np.clip(np.where(amax > 0, np.frexp(amax)[1] - 1 + 127 - 7, 1), 1, 254)
    codes = (b * np.exp2(127.0 - byte)[:, None, :]).reshape(n, m).astype(np.float32).astype(ml_dtypes.float8_e4m3fn).view(np.uint8)
    words = codes.reshape(n // 512, 128, 4, m).transpose(0, 1, 3, 2)
    return np.ascontiguousarray(words), np.ascontiguousarray(byte.astype(np.uint8).reshape(n // 512, 16, m))


N, V, D, Q = 2048, 1024, 512, 1024


def paragraph_vector_model(dv, w, b):
    z = (mxq(dv, 1, "e4m3") @ w) + b[None, :]
    e = np.exp(z - z.max(axis=-1, keepdims=True))
    return e / e.sum(axis=-1, keepdims=True)


def max_likelihood_model(f):
    return f / np.sum(f, axis=-1, keepdims=True)


def log_collection_model(c):
    m = np.max(c)
    return c - (m + np.log(np.sum(np.exp(c - m))))


def setup_inputs():
    s, t = mx_kscale(D), mx_kscale(V)
    dv = bf(np.random.standard_normal((N, D)) * 1.5 * s)
    wv_words, wv_scales = pack4((np.random.standard_normal((V, D)) / np.sqrt(D) / s).T)
    return {
        "dv": dv,
        "wv_words": wv_words,
        "wv_scales": wv_scales,
        "b": bf(0.5 * np.random.standard_normal(V)),
        "f": bf(np.random.uniform(0.0, 2.0, (N, V))),
        "c": bf(0.5 * np.random.standard_normal(V)),
        "g": bf((1.0 + 0.1 * np.random.standard_normal(V)) * t),
        "q": bf(np.random.standard_normal((Q, V)) / np.sqrt(V) / t),
    }


def core(dv, wv_words, wv_scales, b, f, c, g, q):
    dv, b, f, c, g, q = f64(dv), f64(b), f64(f), f64(c), f64(g), f64(q)
    ppv = paragraph_vector_model(dv, unpack4(wv_words, wv_scales), b)
    pml = max_likelihood_model(f)
    pm = 0.5 * ppv + 0.5 * pml
    logpc = log_collection_model(c)
    lr = np.log(pm) - logpc[None, :]
    lg = lr * g[None, :]
    return mxq(q, 1, "e4m3") @ mxq(lg, 1, "e4m3").T


def reference(dv, wv_words, wv_scales, b, f, c, g, q):
    R_out = core(dv, wv_words, wv_scales, b, f, c, g, q)
    words, scales = planes(R_out)
    return R_out, words, scales

@@ -1,0 +1,460 @@
+from contextlib import ExitStack
+
+import concourse.mybir as mybir
+from concourse.masks import make_identity
+
+N_DOCS, N_WORDS, D_MODEL, N_QUERIES = 2048, 1024, 512, 1024
+FLOPS = 2 * N_DOCS * D_MODEL * N_WORDS + 2 * N_QUERIES * N_WORDS * N_DOCS
+
+F32 = mybir.dt.float32
+BF16 = mybir.dt.bfloat16
+I32 = mybir.dt.int32
+U32 = mybir.dt.uint32
+U8 = mybir.dt.uint8
+FP8X4 = mybir.dt.float8_e4m3fn_x4
+FP4X4 = mybir.dt.float4_e2m1fn_x4
+ACT = mybir.ActivationFunctionType
+ALU = mybir.AluOpType
+AX = mybir.AxisListType
+
+P = 128
+PACK = 4
+K_PASS = P * PACK
+BANK = 512
+TILES = N_DOCS // P
+PAIRS = TILES // 2
+WORD_PASSES = N_WORDS // K_PASS
+QUERY_GROUPS = N_QUERIES // K_PASS
+DOC_GROUPS = (2, 2, 2, 2, 2, 2, 2, 1, 1)
+GPSIMD_TILES = 12
+GPSIMD_CHUNK = 512
+FIRST_Q_STEP = 6
+EARLY_SCALES_GROUP = len(DOC_GROUPS) - 4
+
+
+def tile_paragraphvectorsmoothedqueryloglikelihoo_x2_kernel(
+    tc, dv, wv_words, wv_scales, b, f, c, g, q, out_0, out_1, out_2
+):
+    nc = tc.nc
+    with ExitStack() as ctx:
+        keep = ctx.enter_context(tc.tile_pool(name="keep", bufs=1))
+        work = ctx.enter_context(tc.tile_pool(name="work", bufs=2))
+        psum = ctx.enter_context(tc.psum_pool(name="psum", bufs=4))
+        ctx.enter_context(tc.manual_schedule())
+
+        ident = keep.tile([P, P], F32, name="ident")
+        w_codes = keep.tile([P, 2 * N_WORDS], U8, name="w_codes", align_bytes=64)
+        w_scales = keep.tile([P, N_WORDS], U8, name="w_scales", align_bytes=64)
+        dv_codes = keep.tile([P, N_DOCS], U32, name="dv_codes", align_bytes=64)
+        dv_scales = keep.tile([P, N_DOCS], U8, name="dv_scales", align_bytes=64)
+        q_codes = keep.tile([P, WORD_PASSES * N_QUERIES], U32, name="q_codes", align_bytes=64)
+        q_scales = keep.tile([P, WORD_PASSES * N_QUERIES], U8, name="q_scales", align_bytes=64)
+        out_scales = keep.tile([P, QUERY_GROUPS, N_DOCS], U8, name="out_scales", align_bytes=64)
+        b_rows = keep.tile([P, N_WORDS], BF16, name="b_rows")
+        c_cols = keep.tile([P, WORD_PASSES, PACK], BF16, name="c_cols")
+        g_cols = keep.tile([P, WORD_PASSES, PACK], BF16, name="g_cols")
+        shift_cols = keep.tile([P, WORD_PASSES, P], F32, name="shift_cols")
+        shift_rows = keep.tile([P, WORD_PASSES, P], BF16, name="shift_rows")
+        selector = keep.tile([P, PACK, P], BF16, name="selector")
+        warm = keep.tile([P, 1], F32, name="warm")
+        c_part = keep.tile([P, 1], F32, name="c_part")
+        neg_c_max = keep.tile([P, 1], F32, name="neg_c_max")
+        c_exp = keep.tile([P, WORD_PASSES, PACK], F32, name="c_exp")
+        c_exp_part = keep.tile([P, 1], F32, name="c_exp_part")
+        c_exp_sum = keep.tile([P, 1], F32, name="c_exp_sum")
+        neg_max = keep.tile([P, TILES], F32, name="neg_max")
+        exp_sum = keep.tile([P, TILES], F32, name="exp_sum")
+        f_sum = keep.tile([P, TILES], F32, name="f_sum")
+        inv_f_sum = keep.tile([P, TILES], F32, name="inv_f_sum")
+        inv_exp_sum = keep.tile([P, TILES], F32, name="inv_exp_sum")
+        f_ratio = keep.tile([P, TILES], F32, name="f_ratio")
+        ln_scale = keep.tile([P, TILES], F32, name="ln_scale")
+        f_copy = keep.tile([P, N_WORDS], BF16, name="f_copy")
+
+        dv_raw, f_raw, q_raw = {}, {}, {}
+        dv_bank, dv_packed = {}, {}
+        q_bank, q_packed = {}, {}
+        z_bank, rows = {}, {}
+        log_rows, log_bank = {}, {}
+        lg_packed, lg_codes, lg_scales = {}, {}, {}
+        result, result_packed = {}, {}
+        small_bank = {}
+
+        def load_dv(k):
+            dv_raw[k] = keep.tile([P, 2, D_MODEL], BF16, name="dv_raw%d" % k)
+            src = dv[2 * P * k : 2 * P * (k + 1), :].rearrange("(j p) d -> p j d", p=P)
+            nc.sync.dma_start(out=dv_raw[k][:], in_=src)
+
+        def load_f(k):
+            f_raw[k] = work.tile([P, 2, N_WORDS], BF16, name="f_raw", tag="f_or_log", bufs=PAIRS)
+            src = f[2 * P * k : 2 * P * (k + 1), :].rearrange("(j p) v -> p j v", p=P)
+            nc.sync.dma_start(out=f_raw[k][:], in_=src)
+
+        def load_q(gq):
+            q_raw[gq] = work.tile([P, PACK, N_WORDS], BF16, name="q_raw", tag="q_or_result", bufs=3)
+            src = q[K_PASS * gq : K_PASS * (gq + 1), :].rearrange("(m t) v -> m t v", t=PACK)
+            nc.sync.dma_start(out=q_raw[gq][:], in_=src)
+
+        def transpose_words(bank, sources):
+            for j, words in enumerate(sources):
+                for u in range(2):
+                    nc.tensor.transpose(bank[:, j, u, :], words[:, u : 2 * P : 2], ident[:])
+
+        def interleave_words(packed_cols, bank):
+            nc.scalar.copy(
+                out=packed_cols.bitcast(F32).rearrange("p (j r u) -> p j r u", j=2, u=2),
+                in_=bank[:].rearrange("p j u r -> p j r u"),
+            )
+
+        def transpose_dv(k):
+            dv_bank[k] = psum.tile([P, 2, 2, P], F32, name="dv_bank", tag="turn")
+            transpose_words(dv_bank[k], [dv_raw[k][:, j, :].bitcast(F32) for j in range(2)])
+
+        def copy_dv(k):
+            dv_packed[k] = work.tile([P, 2 * P * PACK], BF16, name="dv_packed", tag="packed", bufs=4, align_bytes=64)
+            interleave_words(dv_packed[k][:], dv_bank[k])
+
+        def quantize_dv(k):
+            cols = slice(2 * P * k, 2 * P * (k + 1))
+            nc.vector.quantize_mx(out=dv_codes[:, cols].bitcast(FP8X4), scales=dv_scales[:, cols], in_=dv_packed[k][:])
+
+        def transpose_q(h):
+            unit, half = divmod(h, 2)
+            gq, gw = divmod(unit, WORD_PASSES)
+            q_bank[h] = psum.tile([P, 2, 2, P], F32, name="q_bank", tag="turn")
+            words = slice(K_PASS * gw, K_PASS * (gw + 1))
+            transpose_words(q_bank[h], [q_raw[gq][:, 2 * half + j, words].bitcast(F32) for j in range(2)])
+
+        def copy_q(h):
+            unit, half = divmod(h, 2)
+            if half == 0:
+                q_packed[unit] = work.tile([P, K_PASS * PACK], BF16, name="q_packed", tag="packed", bufs=4, align_bytes=64)
+            interleave_words(q_packed[unit][:, 2 * P * PACK * half : 2 * P * PACK * (half + 1)], q_bank[h])
+
+        def quantize_q(unit):
+            cols = slice(K_PASS * unit, K_PASS * (unit + 1))
+            nc.vector.quantize_mx(out=q_codes[:, cols].bitcast(FP8X4), scales=q_scales[:, cols], in_=q_packed[unit][:])
+
+        def to_slots(natural):
+            return natural.rearrange("p (k t) -> p t k", t=PACK)
+
+        def by_slot(sorted_cols):
+            return sorted_cols.rearrange("p (t k) -> p t k", t=PACK)
+
+        def logits(i):
+            docs = slice(P * i, P * (i + 1))
+            for h in range(2):
+                z_bank[i, h] = psum.tile([P, BANK], F32, name="z_bank", tag="product")
+                nc.tensor.matmul_mx(
+                    out=z_bank[i, h][:],
+                    lhsT=dv_codes[:, docs].bitcast(FP8X4),
+                    lhsT_scale=dv_scales[:, docs],
+                    rhs=w_codes[:, 2 * BANK * h : 2 * BANK * (h + 1)].bitcast(FP4X4),
+                    rhs_scale=w_scales[:, BANK * h : BANK * (h + 1)],
+                    start=True,
+                    stop=True,
+                )
+
+        def add_bias(i):
+            rows[i] = keep.tile([P, N_WORDS], F32, name="row%d" % i)
+            for h in range(2):
+                cols = slice(BANK * h, BANK * (h + 1))
+                nc.vector.scalar_tensor_tensor(
+                    out=by_slot(rows[i][:, cols]), in0=to_slots(z_bank[i, h][:]), scalar=-1.0,
+                    in1=to_slots(b_rows[:, cols]), op0=ALU.mult, op1=ALU.subtract,
+                )
+
+        def row_max(i):
+            nc.vector.tensor_reduce(out=neg_max[:, i : i + 1], in_=rows[i][:], axis=AX.X, op=ALU.min)
+
+        def exponentiate(i):
+            nc.scalar.activation(
+                out=rows[i][:], in_=rows[i][:], func=ACT.Exp, scale=-1.0, bias=neg_max[:, i : i + 1],
+                accum_out=exp_sum[:, i : i + 1],
+            )
+
+        def f_rows(i):
+            return f_raw[i // 2][:, i % 2, :]
+
+        def sum_f(i):
+            nc.scalar.activation(out=f_copy[:], in_=f_rows(i), func=ACT.Identity, accum_out=f_sum[:, i : i + 1])
+
+        def invert_f_sum(k):
+            cols = slice(2 * k, 2 * k + 2)
+            nc.vector.reciprocal(out=inv_f_sum[:, cols], in_=f_sum[:, cols])
+
+        def mix_on_gpsimd(i):
+            for lo in range(0, N_WORDS, GPSIMD_CHUNK):
+                cols = slice(lo, lo + GPSIMD_CHUNK)
+                scaled = work.tile([P, GPSIMD_CHUNK], F32, name="scaled")
+                nc.gpsimd.tensor_scalar(
+                    out=by_slot(scaled[:]), in0=to_slots(f_rows(i)[:, cols]), scalar1=exp_sum[:, i : i + 1],
+                    scalar2=inv_f_sum[:, i : i + 1], op0=ALU.mult, op1=ALU.mult,
+                )
+                nc.gpsimd.tensor_tensor(out=rows[i][:, cols], in0=rows[i][:, cols], in1=scaled[:], op=ALU.add)
+
+        def ratio(lo, hi):
+            nc.vector.tensor_tensor(out=f_ratio[:, lo:hi], in0=exp_sum[:, lo:hi], in1=inv_f_sum[:, lo:hi], op=ALU.mult)
+
+        def mix_on_vector(i):
+            for lo in range(0, N_WORDS, K_PASS):
+                cols = slice(lo, lo + K_PASS)
+                nc.vector.scalar_tensor_tensor(
+                    out=by_slot(rows[i][:, cols]), in0=to_slots(f_rows(i)[:, cols]), scalar=f_ratio[:, i : i + 1],
+                    in1=by_slot(rows[i][:, cols]), op0=ALU.mult, op1=ALU.add,
+                )
+
+        def invert_exp_sum(lo, hi):
+            nc.vector.reciprocal(out=inv_exp_sum[:, lo:hi], in_=exp_sum[:, lo:hi])
+
+        def make_ln_scale(lo, hi):
+            nc.vector.tensor_scalar(
+                out=ln_scale[:, lo:hi], in0=inv_exp_sum[:, lo:hi], scalar1=c_exp_sum[:, 0:1], scalar2=0.5,
+                op0=ALU.mult, op1=ALU.mult,
+            )
+
+        def spread(name, column):
+            small_bank[name] = psum.tile([P, P], F32, name="spread_bank", tag="turn")
+            nc.tensor.transpose(small_bank[name][:], column.to_broadcast([P, P]), ident[:])
+
+        neg_c = shift_cols[:, :, 0:PACK]
+
+        def c_step(s):
+            if s == 0:
+                nc.vector.tensor_scalar(out=neg_c, in0=c_cols[:], scalar1=-1.0, scalar2=None, op0=ALU.mult)
+            elif s == 1:
+                nc.vector.tensor_reduce(out=c_part[:], in_=neg_c, axis=AX.XY, op=ALU.min)
+                spread("max", c_part[:, 0:1])
+            elif s == 2:
+                nc.vector.tensor_reduce(out=neg_c_max[:], in_=small_bank["max"][:], axis=AX.X, op=ALU.min)
+            elif s == 3:
+                nc.vector.tensor_scalar(
+                    out=shift_cols[:, :, PACK], in0=neg_c_max[:, 0:1].to_broadcast([P, WORD_PASSES]),
+                    scalar1=-1.0, scalar2=None, op0=ALU.mult,
+                )
+                nc.scalar.activation(
+                    out=c_exp[:], in_=neg_c, func=ACT.Exp, scale=-1.0, bias=neg_c_max[:, 0:1], accum_out=c_exp_part[:]
+                )
+            elif s == 4:
+                spread("sum", c_exp_part[:, 0:1])
+                small_bank["rows"] = psum.tile([P, WORD_PASSES, P], F32, name="shift_bank", tag="turn")
+                for gw in range(WORD_PASSES):
+                    nc.tensor.transpose(small_bank["rows"][:, gw, :], shift_cols[:, gw, :], ident[:])
+            elif s == 5:
+                nc.vector.tensor_reduce(out=c_exp_sum[:], in_=small_bank["sum"][:], axis=AX.X, op=ALU.add)
+                nc.scalar.copy(out=shift_rows[:], in_=small_bank["rows"][:])
+
+        def logarithm(i):
+            log_rows[i] = work.tile([P, N_WORDS], F32, name="log_rows", tag="f_or_log", bufs=PAIRS)
+            nc.scalar.activation(
+                out=log_rows[i][:],
+                in_=rows[i][:],
+                func=ACT.Ln,
+                scale=ln_scale[:, i : i + 1],
+            )
+
+        def transpose_log(i):
+            for gw in range(WORD_PASSES):
+                log_bank[i, gw] = psum.tile([P, PACK, P], F32, name="log_bank", tag="turn")
+                nc.tensor.matmul(
+                    log_bank[i, gw][:].rearrange("p t n -> p (t n)"), lhsT=shift_rows[:, gw, :],
+                    rhs=selector[:].rearrange("p t n -> p (t n)"), start=True, stop=False,
+                )
+            for gw in range(WORD_PASSES):
+                for t in range(PACK):
+                    lo = K_PASS * gw + P * t
+                    nc.tensor.matmul(
+                        log_bank[i, gw][:, t, :], lhsT=log_rows[i][:, lo : lo + P], rhs=ident[:],
+                        is_transpose=True, start=False, stop=(t == PACK - 1),
+                    )
+
+        group_start = [sum(DOC_GROUPS[:k]) for k in range(len(DOC_GROUPS))]
+        group_of = [k for k, size in enumerate(DOC_GROUPS) for j in range(size)]
+
+        def apply_gain(i, gw):
+            k = group_of[i]
+            j = i - group_start[k]
+            if j == 0:
+                lg_packed[k, gw] = work.tile(
+                    [P, DOC_GROUPS[k] * P * PACK], BF16, name="lg_packed", tag="packed", bufs=4, align_bytes=64
+                )
+            nc.vector.tensor_tensor(
+                out=lg_packed[k, gw][:, BANK * j : BANK * (j + 1)].rearrange("p (n t) -> p n t", t=PACK),
+                in0=log_bank[i, gw][:].rearrange("p t n -> p n t"),
+                in1=g_cols[:, gw, :].unsqueeze(1).to_broadcast([P, P, PACK]),
+                op=ALU.mult,
+            )
+
+        def quantize_lg(k):
+            width = DOC_GROUPS[k] * P
+            for gw in range(WORD_PASSES):
+                lg_codes[k, gw] = work.tile([P, width], U32, name="lg_codes", bufs=4, align_bytes=64)
+                lg_scales[k, gw] = work.tile([P, width], U8, name="lg_scales", bufs=4, align_bytes=64)
+                nc.vector.quantize_mx(
+                    out=lg_codes[k, gw][:].bitcast(FP8X4), scales=lg_scales[k, gw][:], in_=lg_packed[k, gw][:]
+                )
+
+        def doc_cols(k):
+            return slice(P * group_start[k], P * (group_start[k] + DOC_GROUPS[k]))
+
+        def scores(k, gq, r, on_vector):
+            width = DOC_GROUPS[k] * P
+            slots = BANK // width
+            if r == 0:
+                result[k, gq] = work.tile([P, PACK * width], F32, name="result", tag="q_or_result", bufs=3)
+            bank = psum.tile([P, BANK], F32, name="score_bank", tag="product")
+            for s in range(slots):
+                t = slots * r + s
+                for gw in range(WORD_PASSES):
+                    lo = K_PASS * (WORD_PASSES * gq + gw) + P * t
+                    nc.tensor.matmul_mx(
+                        out=bank[:, width * s : width * (s + 1)],
+                        lhsT=q_codes[:, lo : lo + P].bitcast(FP8X4),
+                        lhsT_scale=q_scales[:, lo : lo + P],
+                        rhs=lg_codes[k, gw][:].bitcast(FP8X4),
+                        rhs_scale=lg_scales[k, gw][:],
+                        start=(gw == 0),
+                        stop=(gw == WORD_PASSES - 1),
+                    )
+            dst = result[k, gq][:, BANK * r : BANK * (r + 1)]
+            if on_vector:
+                nc.vector.tensor_copy(out=dst, in_=bank[:])
+            else:
+                nc.scalar.copy(out=dst, in_=bank[:])
+
+        def store_result(k, gq):
+            dst = out_0[K_PASS * gq : K_PASS * (gq + 1), doc_cols(k)].rearrange("(p t) m -> p t m", t=PACK)
+            nc.sync.dma_start(out=dst, in_=result[k, gq][:].rearrange("p (t m) -> p t m", t=PACK))
+
+        def pack_result(k, gq):
+            width = DOC_GROUPS[k] * P
+            result_packed[k, gq] = work.tile([P, width * PACK], BF16, name="result_packed", align_bytes=64)
+            nc.vector.tensor_copy(
+                out=result_packed[k, gq][:].rearrange("p (m t) -> p m t", t=PACK),
+                in_=result[k, gq][:].rearrange("p (t m) -> p m t", t=PACK),
+            )
+
+        def quantize_result(k, gq):
+            codes = work.tile([P, DOC_GROUPS[k] * P], U32, name="result_codes", bufs=3, align_bytes=64)
+            nc.vector.quantize_mx(
+                out=codes[:].bitcast(FP8X4), scales=out_scales[:, gq, doc_cols(k)], in_=result_packed[k, gq][:]
+            )
+            dst = out_1[gq, :, doc_cols(k), :].rearrange("p m t -> p (m t)").bitcast(I32)
+            nc.sync.dma_start(out=dst, in_=codes[:].bitcast(I32))
+
+        def store_scales(cols):
+            for quad in range(4):
+                dst = out_2[:, 4 * quad : 4 * quad + 4, cols].rearrange("g r m -> r g m").bitcast(I32)
+                nc.sync.dma_start(out=dst, in_=out_scales[32 * quad : 32 * quad + 4, :, cols].bitcast(I32))
+
+        nc.vector.memset(w_scales[:].bitcast(I32), 0)
+        nc.vector.memset(warm[:], 0.0)
+        nc.scalar.dma_start(out=b_rows[:], in_=b.partition_broadcast(P))
+        nc.scalar.activation(out=warm[:], in_=warm[:], func=ACT.Exp)
+        make_identity(nc, ident[:])
+        load_dv(0)
+        nc.sync.dma_start(out=w_codes[:].bitcast(I32), in_=wv_words[0].bitcast(I32))
+        for quad in range(4):
+            nc.sync.dma_start(
+                out=w_scales[32 * quad : 32 * quad + 4, :].bitcast(I32),
+                in_=wv_scales[0, 4 * quad : 4 * quad + 4, :].bitcast(I32),
+            )
+        load_dv(1)
+        load_f(0)
+        nc.sync.dma_start(out=c_cols[:], in_=c.rearrange("(w p t) -> p w t", p=P, t=PACK))
+        nc.sync.dma_start(out=g_cols[:], in_=g.rearrange("(w p t) -> p w t", p=P, t=PACK))
+        for k in range(1, PAIRS):
+            if k + 1 < PAIRS:
+                load_dv(k + 1)
+            load_f(k)
+            if k in (2, 4):
+                load_q(k // 2 - 1)
+        nc.vector.memset(shift_cols[:], 0.0)
+        nc.vector.tensor_tensor(
+            out=selector[:],
+            in0=ident[:, 0:PACK].unsqueeze(2).to_broadcast([P, PACK, P]),
+            in1=ident[:, PACK : PACK + 1].unsqueeze(2).to_broadcast([P, PACK, P]),
+            op=ALU.add,
+        )
+        transpose_dv(0)
+        copy_dv(0)
+        quantize_dv(0)
+        transpose_dv(1)
+        logits(0)
+        copy_dv(1)
+        sum_f(0)
+
+        for i in range(TILES + 1):
+            if i % 2 == 1 and (i + 3) // 2 < PAIRS:
+                transpose_dv((i + 3) // 2)
+            if 0 <= i - FIRST_Q_STEP < 8:
+                transpose_q(i - FIRST_Q_STEP)
+            if i + 1 < TILES:
+                if i % 2 == 1:
+                    quantize_dv((i + 1) // 2)
+                logits(i + 1)
+            if i < TILES:
+                add_bias(i)
+            if i % 2 == 0 and 2 <= (i + 2) // 2 < PAIRS:
+                copy_dv((i + 2) // 2)
+            if 0 <= i - FIRST_Q_STEP - 1 < 8:
+                copy_q(i - FIRST_Q_STEP - 1)
+            if i + 1 < TILES:
+                sum_f(i + 1)
+            if i >= 1:
+                row_max(i - 1)
+                exponentiate(i - 1)
+            if i % 2 == 1:
+                invert_f_sum(i // 2)
+            if 0 <= i - FIRST_Q_STEP - 3 < 8 and (i - FIRST_Q_STEP - 3) % 2 == 0:
+                quantize_q((i - FIRST_Q_STEP - 3) // 2)
+            c_step(i - 1)
+            if 0 <= i - 1 < GPSIMD_TILES:
+                mix_on_gpsimd(i - 1)
+            if i == TILES - 2:
+                invert_exp_sum(0, GPSIMD_TILES)
+            if i == TILES - 1:
+                make_ln_scale(0, GPSIMD_TILES)
+
+        ratio(GPSIMD_TILES, TILES - 1)
+        logarithm(0)
+        for i in range(GPSIMD_TILES, TILES - 1):
+            mix_on_vector(i)
+        ratio(TILES - 1, TILES)
+        invert_exp_sum(GPSIMD_TILES, TILES)
+        mix_on_vector(TILES - 1)
+        make_ln_scale(GPSIMD_TILES, TILES)
+        logarithm(1)
+        transpose_log(0)
+
+        banks, to_pack, to_quantize = [], [], []
+        step = 0
+        while step < TILES + 1 or banks or to_pack or to_quantize:
+            if step + 2 < TILES:
+                logarithm(step + 2)
+            if step + 1 < TILES:
+                transpose_log(step + 1)
+            if step < TILES:
+                apply_gain(step, 0)
+            if step >= 1 and step - 1 < TILES and (step == TILES or group_of[step] != group_of[step - 1]):
+                k = group_of[step - 1]
+                quantize_lg(k)
+                banks.extend((k, gq, r) for gq in range(QUERY_GROUPS) for r in range(DOC_GROUPS[k]))
+            if step < TILES:
+                apply_gain(step, 1)
+            for k, gq in to_quantize:
+                quantize_result(k, gq)
+                if gq == QUERY_GROUPS - 1 and k == EARLY_SCALES_GROUP:
+                    store_scales(slice(0, doc_cols(k).stop))
+            to_quantize = to_pack
+            for k, gq in to_pack:
+                pack_result(k, gq)
+            to_pack = []
+            for j, (k, gq, r) in enumerate(banks[:2]):
+                scores(k, gq, r, False)
+                if r == DOC_GROUPS[k] - 1:
+                    store_result(k, gq)
+                    to_pack.append((k, gq))
+            banks = banks[2:]
+            step += 1
+        store_scales(slice(doc_cols(EARLY_SCALES_GROUP).stop, N_DOCS))

@@ -25,11 +25,14 @@ TILES = N_DOCS // P
 PAIRS = TILES // 2
 WORD_PASSES = N_WORDS // K_PASS
 QUERY_GROUPS = N_QUERIES // K_PASS
-DOC_GROUPS = (2, 2, 2, 2, 2, 2, 2, 1, 1)
-GPSIMD_TILES = 12
-GPSIMD_CHUNK = 512
+MIX_LEAD = 4
+F_SUM_LEAD = 2
+VECTOR_F_SUMS = (9, 11, 13)
+EARLY_STATS = 8
+SCALAR_PACKS_BOTH = 3
+SCALAR_PACKS_ONE = 16
 FIRST_Q_STEP = 6
-EARLY_SCALES_GROUP = len(DOC_GROUPS) - 4
+EARLY_SCALE_PAIRS = 4
 
 
 def tile_paragraphvectorsmoothedqueryloglikelihoo_x2_kernel(
@@ -49,7 +52,9 @@ def tile_paragraphvectorsmoothedqueryloglikelihoo_x2_kernel(
         dv_scales = keep.tile([P, N_DOCS], U8, name="dv_scales", align_bytes=64)
         q_codes = keep.tile([P, WORD_PASSES * N_QUERIES], U32, name="q_codes", align_bytes=64)
         q_scales = keep.tile([P, WORD_PASSES * N_QUERIES], U8, name="q_scales", align_bytes=64)
-        out_scales = keep.tile([P, QUERY_GROUPS, N_DOCS], U8, name="out_scales", align_bytes=64)
+        early_docs = 2 * P * EARLY_SCALE_PAIRS
+        early_scales = keep.tile([P, QUERY_GROUPS, early_docs], U8, name="early_scales", align_bytes=64)
+        late_scales = keep.tile([P, QUERY_GROUPS, N_DOCS - early_docs], U8, name="late_scales", align_bytes=64)
         b_rows = keep.tile([P, N_WORDS], BF16, name="b_rows")
         c_cols = keep.tile([P, WORD_PASSES, PACK], BF16, name="c_cols")
         g_cols = keep.tile([P, WORD_PASSES, PACK], BF16, name="g_cols")
@@ -63,19 +68,20 @@ def tile_paragraphvectorsmoothedqueryloglikelihoo_x2_kernel(
         c_exp_part = keep.tile([P, 1], F32, name="c_exp_part")
         c_exp_sum = keep.tile([P, 1], F32, name="c_exp_sum")
         neg_max = keep.tile([P, TILES], F32, name="neg_max")
-        exp_sum = keep.tile([P, TILES], F32, name="exp_sum")
-        f_sum = keep.tile([P, TILES], F32, name="f_sum")
-        inv_f_sum = keep.tile([P, TILES], F32, name="inv_f_sum")
-        inv_exp_sum = keep.tile([P, TILES], F32, name="inv_exp_sum")
+        sums = keep.tile([P, TILES, 2], F32, name="sums")
+        inv_sums = keep.tile([P, TILES, 2], F32, name="inv_sums")
+        exp_sum, f_sum = sums[:, :, 0], sums[:, :, 1]
+        inv_exp_sum, inv_f_sum = inv_sums[:, :, 0], inv_sums[:, :, 1]
         f_ratio = keep.tile([P, TILES], F32, name="f_ratio")
         ln_scale = keep.tile([P, TILES], F32, name="ln_scale")
+        f_copy_v = keep.tile([P, N_WORDS], BF16, name="f_copy_v")
         f_copy = keep.tile([P, N_WORDS], BF16, name="f_copy")
 
         dv_raw, f_raw, q_raw = {}, {}, {}
         dv_bank, dv_packed = {}, {}
         q_bank, q_packed = {}, {}
         z_bank, rows = {}, {}
-        log_rows, log_bank = {}, {}
+        log_bank, score_bank = {}, {}
         lg_packed, lg_codes, lg_scales = {}, {}, {}
         result, result_packed = {}, {}
         small_bank = {}
@@ -86,12 +92,12 @@ def tile_paragraphvectorsmoothedqueryloglikelihoo_x2_kernel(
             nc.sync.dma_start(out=dv_raw[k][:], in_=src)
 
         def load_f(k):
-            f_raw[k] = work.tile([P, 2, N_WORDS], BF16, name="f_raw", tag="f_or_log", bufs=PAIRS)
+            f_raw[k] = keep.tile([P, 2, N_WORDS], BF16, name="f_raw%d" % k)
             src = f[2 * P * k : 2 * P * (k + 1), :].rearrange("(j p) v -> p j v", p=P)
             nc.sync.dma_start(out=f_raw[k][:], in_=src)
 
         def load_q(gq):
-            q_raw[gq] = work.tile([P, PACK, N_WORDS], BF16, name="q_raw", tag="q_or_result", bufs=3)
+            q_raw[gq] = keep.tile([P, PACK, N_WORDS], BF16, name="q_raw%d" % gq)
             src = q[K_PASS * gq : K_PASS * (gq + 1), :].rearrange("(m t) v -> m t v", t=PACK)
             nc.sync.dma_start(out=q_raw[gq][:], in_=src)
 
@@ -111,7 +117,7 @@ def tile_paragraphvectorsmoothedqueryloglikelihoo_x2_kernel(
             transpose_words(dv_bank[k], [dv_raw[k][:, j, :].bitcast(F32) for j in range(2)])
 
         def copy_dv(k):
-            dv_packed[k] = work.tile([P, 2 * P * PACK], BF16, name="dv_packed", tag="packed", bufs=4, align_bytes=64)
+            dv_packed[k] = work.tile([P, 2 * P * PACK], BF16, name="dv_packed", tag="packed", bufs=6, align_bytes=64)
             interleave_words(dv_packed[k][:], dv_bank[k])
 
         def quantize_dv(k):
@@ -128,7 +134,7 @@ def tile_paragraphvectorsmoothedqueryloglikelihoo_x2_kernel(
         def copy_q(h):
             unit, half = divmod(h, 2)
             if half == 0:
-                q_packed[unit] = work.tile([P, K_PASS * PACK], BF16, name="q_packed", tag="packed", bufs=4, align_bytes=64)
+                q_packed[unit] = work.tile([P, K_PASS * PACK], BF16, name="q_packed", tag="packed", bufs=6, align_bytes=64)
             interleave_words(q_packed[unit][:, 2 * P * PACK * half : 2 * P * PACK * (half + 1)], q_bank[h])
 
         def quantize_q(unit):
@@ -177,35 +183,26 @@ def tile_paragraphvectorsmoothedqueryloglikelihoo_x2_kernel(
             return f_raw[i // 2][:, i % 2, :]
 
         def sum_f(i):
-            nc.scalar.activation(out=f_copy[:], in_=f_rows(i), func=ACT.Identity, accum_out=f_sum[:, i : i + 1])
-
-        def invert_f_sum(k):
-            cols = slice(2 * k, 2 * k + 2)
-            nc.vector.reciprocal(out=inv_f_sum[:, cols], in_=f_sum[:, cols])
-
-        def mix_on_gpsimd(i):
-            for lo in range(0, N_WORDS, GPSIMD_CHUNK):
-                cols = slice(lo, lo + GPSIMD_CHUNK)
-                scaled = work.tile([P, GPSIMD_CHUNK], F32, name="scaled")
-                nc.gpsimd.tensor_scalar(
-                    out=by_slot(scaled[:]), in0=to_slots(f_rows(i)[:, cols]), scalar1=exp_sum[:, i : i + 1],
-                    scalar2=inv_f_sum[:, i : i + 1], op0=ALU.mult, op1=ALU.mult,
+            if i in VECTOR_F_SUMS:
+                nc.vector.tensor_scalar(
+                    out=f_copy_v[:], in0=f_rows(i), scalar1=1.0, scalar2=None, op0=ALU.mult, op1=ALU.add,
+                    accum_out=f_sum[:, i : i + 1],
                 )
-                nc.gpsimd.tensor_tensor(out=rows[i][:, cols], in0=rows[i][:, cols], in1=scaled[:], op=ALU.add)
+            else:
+                nc.scalar.activation(out=f_copy[:], in_=f_rows(i), func=ACT.Identity, accum_out=f_sum[:, i : i + 1])
 
         def ratio(lo, hi):
             nc.vector.tensor_tensor(out=f_ratio[:, lo:hi], in0=exp_sum[:, lo:hi], in1=inv_f_sum[:, lo:hi], op=ALU.mult)
 
-        def mix_on_vector(i):
-            for lo in range(0, N_WORDS, K_PASS):
-                cols = slice(lo, lo + K_PASS)
-                nc.vector.scalar_tensor_tensor(
-                    out=by_slot(rows[i][:, cols]), in0=to_slots(f_rows(i)[:, cols]), scalar=f_ratio[:, i : i + 1],
-                    in1=by_slot(rows[i][:, cols]), op0=ALU.mult, op1=ALU.add,
-                )
+        def mix(i, gw):
+            cols = slice(K_PASS * gw, K_PASS * (gw + 1))
+            nc.vector.scalar_tensor_tensor(
+                out=by_slot(rows[i][:, cols]), in0=to_slots(f_rows(i)[:, cols]), scalar=f_ratio[:, i : i + 1],
+                in1=by_slot(rows[i][:, cols]), op0=ALU.mult, op1=ALU.add,
+            )
 
-        def invert_exp_sum(lo, hi):
-            nc.vector.reciprocal(out=inv_exp_sum[:, lo:hi], in_=exp_sum[:, lo:hi])
+        def invert_sums(lo, hi):
+            nc.vector.reciprocal(out=inv_sums[:, lo:hi, :], in_=sums[:, lo:hi, :])
 
         def make_ln_scale(lo, hi):
             nc.vector.tensor_scalar(
@@ -245,13 +242,7 @@ def tile_paragraphvectorsmoothedqueryloglikelihoo_x2_kernel(
                 nc.scalar.copy(out=shift_rows[:], in_=small_bank["rows"][:])
 
         def logarithm(i):
-            log_rows[i] = work.tile([P, N_WORDS], F32, name="log_rows", tag="f_or_log", bufs=PAIRS)
-            nc.scalar.activation(
-                out=log_rows[i][:],
-                in_=rows[i][:],
-                func=ACT.Ln,
-                scale=ln_scale[:, i : i + 1],
-            )
+            nc.scalar.activation(out=rows[i][:], in_=rows[i][:], func=ACT.Ln, scale=ln_scale[:, i : i + 1])
 
         def transpose_log(i):
             for gw in range(WORD_PASSES):
@@ -264,88 +255,86 @@ def tile_paragraphvectorsmoothedqueryloglikelihoo_x2_kernel(
                 for t in range(PACK):
                     lo = K_PASS * gw + P * t
                     nc.tensor.matmul(
-                        log_bank[i, gw][:, t, :], lhsT=log_rows[i][:, lo : lo + P], rhs=ident[:],
+                        log_bank[i, gw][:, t, :], lhsT=rows[i][:, lo : lo + P], rhs=ident[:],
                         is_transpose=True, start=False, stop=(t == PACK - 1),
                     )
 
-        group_start = [sum(DOC_GROUPS[:k]) for k in range(len(DOC_GROUPS))]
-        group_of = [k for k, size in enumerate(DOC_GROUPS) for j in range(size)]
-
         def apply_gain(i, gw):
-            k = group_of[i]
-            j = i - group_start[k]
-            if j == 0:
-                lg_packed[k, gw] = work.tile(
-                    [P, DOC_GROUPS[k] * P * PACK], BF16, name="lg_packed", tag="packed", bufs=4, align_bytes=64
-                )
+            if gw == 0:
+                lg_packed[i] = work.tile([P, N_WORDS], BF16, name="lg_packed", tag="packed", bufs=6, align_bytes=64)
             nc.vector.tensor_tensor(
-                out=lg_packed[k, gw][:, BANK * j : BANK * (j + 1)].rearrange("p (n t) -> p n t", t=PACK),
+                out=lg_packed[i][:, BANK * gw : BANK * (gw + 1)].rearrange("p (n t) -> p n t", t=PACK),
                 in0=log_bank[i, gw][:].rearrange("p t n -> p n t"),
                 in1=g_cols[:, gw, :].unsqueeze(1).to_broadcast([P, P, PACK]),
                 op=ALU.mult,
             )
 
-        def quantize_lg(k):
-            width = DOC_GROUPS[k] * P
-            for gw in range(WORD_PASSES):
-                lg_codes[k, gw] = work.tile([P, width], U32, name="lg_codes", bufs=4, align_bytes=64)
-                lg_scales[k, gw] = work.tile([P, width], U8, name="lg_scales", bufs=4, align_bytes=64)
-                nc.vector.quantize_mx(
-                    out=lg_codes[k, gw][:].bitcast(FP8X4), scales=lg_scales[k, gw][:], in_=lg_packed[k, gw][:]
-                )
+        def quantize_lg(i):
+            lg_codes[i] = work.tile([P, WORD_PASSES * P], U32, name="lg_codes", bufs=3, align_bytes=64)
+            lg_scales[i] = work.tile([P, WORD_PASSES * P], U8, name="lg_scales", bufs=3, align_bytes=64)
+            nc.vector.quantize_mx(out=lg_codes[i][:].bitcast(FP8X4), scales=lg_scales[i][:], in_=lg_packed[i][:])
 
         def doc_cols(k):
-            return slice(P * group_start[k], P * (group_start[k] + DOC_GROUPS[k]))
+            return slice(2 * P * k, 2 * P * (k + 1))
 
-        def scores(k, gq, r, on_vector):
-            width = DOC_GROUPS[k] * P
-            slots = BANK // width
-            if r == 0:
-                result[k, gq] = work.tile([P, PACK * width], F32, name="result", tag="q_or_result", bufs=3)
-            bank = psum.tile([P, BANK], F32, name="score_bank", tag="product")
-            for s in range(slots):
-                t = slots * r + s
+        def scores(i, gq):
+            score_bank[i, gq] = psum.tile([P, PACK, P], F32, name="score_bank", tag="product")
+            for t in range(PACK):
                 for gw in range(WORD_PASSES):
                     lo = K_PASS * (WORD_PASSES * gq + gw) + P * t
                     nc.tensor.matmul_mx(
-                        out=bank[:, width * s : width * (s + 1)],
+                        out=score_bank[i, gq][:, t, :],
                         lhsT=q_codes[:, lo : lo + P].bitcast(FP8X4),
                         lhsT_scale=q_scales[:, lo : lo + P],
-                        rhs=lg_codes[k, gw][:].bitcast(FP8X4),
-                        rhs_scale=lg_scales[k, gw][:],
+                        rhs=lg_codes[i][:, P * gw : P * (gw + 1)].bitcast(FP8X4),
+                        rhs_scale=lg_scales[i][:, P * gw : P * (gw + 1)],
                         start=(gw == 0),
                         stop=(gw == WORD_PASSES - 1),
                     )
-            dst = result[k, gq][:, BANK * r : BANK * (r + 1)]
-            if on_vector:
-                nc.vector.tensor_copy(out=dst, in_=bank[:])
+
+        def store_group(i):
+            return range(i, i + 1) if i >= TILES - 2 else range(i - i % 2, i - i % 2 + 2)
+
+        def result_cols(i, gq):
+            lo = store_group(i).start
+            return result[lo, gq][:, :, P * (i - lo) : P * (i - lo + 1)]
+
+        def copy_scores(i, gq):
+            if i == store_group(i).start:
+                result[i, gq] = work.tile([P, PACK, len(store_group(i)) * P], F32, name="result", bufs=6)
+            nc.scalar.copy(out=result_cols(i, gq), in_=score_bank[i, gq][:])
+
+        def pack_result(i, gq, on_scalar):
+            k, j = divmod(i, 2)
+            if j == 0:
+                result_packed[k, gq] = work.tile([P, 2 * BANK], BF16, name="result_packed", bufs=4, align_bytes=64)
+            dst = result_packed[k, gq][:, BANK * j : BANK * (j + 1)].rearrange("p (m t) -> p m t", t=PACK)
+            if on_scalar:
+                nc.scalar.copy(out=dst, in_=score_bank[i, gq][:].rearrange("p t m -> p m t"))
             else:
-                nc.scalar.copy(out=dst, in_=bank[:])
+                nc.vector.tensor_copy(out=dst, in_=result_cols(i, gq).rearrange("p t m -> p m t"))
 
-        def store_result(k, gq):
-            dst = out_0[K_PASS * gq : K_PASS * (gq + 1), doc_cols(k)].rearrange("(p t) m -> p t m", t=PACK)
-            nc.sync.dma_start(out=dst, in_=result[k, gq][:].rearrange("p (t m) -> p t m", t=PACK))
+        def store_result(tiles, gq):
+            docs = slice(P * tiles.start, P * tiles.stop)
+            dst = out_0[K_PASS * gq : K_PASS * (gq + 1), docs].rearrange("(p t) m -> p t m", t=PACK)
+            nc.sync.dma_start(out=dst, in_=result[tiles.start, gq][:])
 
-        def pack_result(k, gq):
-            width = DOC_GROUPS[k] * P
-            result_packed[k, gq] = work.tile([P, width * PACK], BF16, name="result_packed", align_bytes=64)
-            nc.vector.tensor_copy(
-                out=result_packed[k, gq][:].rearrange("p (m t) -> p m t", t=PACK),
-                in_=result[k, gq][:].rearrange("p (t m) -> p m t", t=PACK),
-            )
-
-        def quantize_result(k, gq):
-            codes = work.tile([P, DOC_GROUPS[k] * P], U32, name="result_codes", bufs=3, align_bytes=64)
-            nc.vector.quantize_mx(
-                out=codes[:].bitcast(FP8X4), scales=out_scales[:, gq, doc_cols(k)], in_=result_packed[k, gq][:]
-            )
-            dst = out_1[gq, :, doc_cols(k), :].rearrange("p m t -> p (m t)").bitcast(I32)
+        def quantize_result(k):
+            cols = doc_cols(k)
+            codes = work.tile([P, QUERY_GROUPS, 2 * P], U32, name="result_codes", bufs=3, align_bytes=64)
+            for gq in range(QUERY_GROUPS):
+                if k < EARLY_SCALE_PAIRS:
+                    scales = early_scales[:, gq, cols]
+                else:
+                    scales = late_scales[:, gq, cols.start - early_docs : cols.stop - early_docs]
+                nc.vector.quantize_mx(out=codes[:, gq, :].bitcast(FP8X4), scales=scales, in_=result_packed[k, gq][:])
+            dst = out_1[:, :, cols, :].rearrange("g p m t -> p g (m t)").bitcast(I32)
             nc.sync.dma_start(out=dst, in_=codes[:].bitcast(I32))
 
-        def store_scales(cols):
+        def store_scales(queue, scales, cols):
             for quad in range(4):
                 dst = out_2[:, 4 * quad : 4 * quad + 4, cols].rearrange("g r m -> r g m").bitcast(I32)
-                nc.sync.dma_start(out=dst, in_=out_scales[32 * quad : 32 * quad + 4, :, cols].bitcast(I32))
+                queue.dma_start(out=dst, in_=scales[32 * quad : 32 * quad + 4, :, :].bitcast(I32))
 
         nc.vector.memset(w_scales[:].bitcast(I32), 0)
         nc.vector.memset(warm[:], 0.0)
@@ -361,13 +350,16 @@ def tile_paragraphvectorsmoothedqueryloglikelihoo_x2_kernel(
             )
         load_dv(1)
         load_f(0)
+        load_dv(2)
+        load_f(1)
+        load_dv(3)
         nc.sync.dma_start(out=c_cols[:], in_=c.rearrange("(w p t) -> p w t", p=P, t=PACK))
         nc.sync.dma_start(out=g_cols[:], in_=g.rearrange("(w p t) -> p w t", p=P, t=PACK))
-        for k in range(1, PAIRS):
-            if k + 1 < PAIRS:
-                load_dv(k + 1)
+        for k in range(2, PAIRS):
             load_f(k)
-            if k in (2, 4):
+            if k + 2 < PAIRS:
+                load_dv(k + 2)
+            if k in (3, 5):
                 load_q(k // 2 - 1)
         nc.vector.memset(shift_cols[:], 0.0)
         nc.vector.tensor_tensor(
@@ -379,14 +371,16 @@ def tile_paragraphvectorsmoothedqueryloglikelihoo_x2_kernel(
         transpose_dv(0)
         copy_dv(0)
         quantize_dv(0)
-        transpose_dv(1)
         logits(0)
+        transpose_dv(1)
         copy_dv(1)
-        sum_f(0)
+        for i in range(F_SUM_LEAD - 1):
+            sum_f(i)
+        transpose_dv(2)
 
         for i in range(TILES + 1):
-            if i % 2 == 1 and (i + 3) // 2 < PAIRS:
-                transpose_dv((i + 3) // 2)
+            if i % 2 == 1 and (i + 5) // 2 < PAIRS:
+                transpose_dv((i + 5) // 2)
             if 0 <= i - FIRST_Q_STEP < 8:
                 transpose_q(i - FIRST_Q_STEP)
             if i + 1 < TILES:
@@ -395,66 +389,66 @@ def tile_paragraphvectorsmoothedqueryloglikelihoo_x2_kernel(
                 logits(i + 1)
             if i < TILES:
                 add_bias(i)
-            if i % 2 == 0 and 2 <= (i + 2) // 2 < PAIRS:
-                copy_dv((i + 2) // 2)
+            if i % 2 == 0 and (i + 4) // 2 < PAIRS:
+                copy_dv((i + 4) // 2)
             if 0 <= i - FIRST_Q_STEP - 1 < 8:
                 copy_q(i - FIRST_Q_STEP - 1)
-            if i + 1 < TILES:
-                sum_f(i + 1)
+            if i + F_SUM_LEAD - 1 < TILES:
+                sum_f(i + F_SUM_LEAD - 1)
             if i >= 1:
                 row_max(i - 1)
                 exponentiate(i - 1)
-            if i % 2 == 1:
-                invert_f_sum(i // 2)
-            if 0 <= i - FIRST_Q_STEP - 3 < 8 and (i - FIRST_Q_STEP - 3) % 2 == 0:
-                quantize_q((i - FIRST_Q_STEP - 3) // 2)
+            if 0 <= i - FIRST_Q_STEP - 4 < 8 and (i - FIRST_Q_STEP - 4) % 2 == 0:
+                quantize_q((i - FIRST_Q_STEP - 4) // 2)
             c_step(i - 1)
-            if 0 <= i - 1 < GPSIMD_TILES:
-                mix_on_gpsimd(i - 1)
+            if i == TILES - 3:
+                invert_sums(0, EARLY_STATS)
             if i == TILES - 2:
-                invert_exp_sum(0, GPSIMD_TILES)
+                ratio(0, EARLY_STATS)
+                make_ln_scale(0, EARLY_STATS)
             if i == TILES - 1:
-                make_ln_scale(0, GPSIMD_TILES)
+                mix(0, 0)
+                mix(0, 1)
 
-        ratio(GPSIMD_TILES, TILES - 1)
         logarithm(0)
-        for i in range(GPSIMD_TILES, TILES - 1):
-            mix_on_vector(i)
-        ratio(TILES - 1, TILES)
-        invert_exp_sum(GPSIMD_TILES, TILES)
-        mix_on_vector(TILES - 1)
-        make_ln_scale(GPSIMD_TILES, TILES)
+        for i in range(1, MIX_LEAD):
+            mix(i, 0)
+            mix(i, 1)
+        invert_sums(EARLY_STATS, TILES)
         logarithm(1)
         transpose_log(0)
 
-        banks, to_pack, to_quantize = [], [], []
-        step = 0
-        while step < TILES + 1 or banks or to_pack or to_quantize:
+        def scalar_packs(i, gq):
+            return i < SCALAR_PACKS_BOTH or (i < SCALAR_PACKS_ONE and gq == 1)
+
+        for step in range(TILES + 4):
             if step + 2 < TILES:
                 logarithm(step + 2)
             if step + 1 < TILES:
                 transpose_log(step + 1)
+            for gq in range(QUERY_GROUPS):
+                if 0 <= step - 1 < TILES:
+                    scores(step - 1, gq)
+                    copy_scores(step - 1, gq)
+                    if scalar_packs(step - 1, gq):
+                        pack_result(step - 1, gq, True)
+                    if step == store_group(step - 1).stop:
+                        store_result(store_group(step - 1), gq)
+            for gw in range(WORD_PASSES):
+                if step < TILES:
+                    apply_gain(step, gw)
+                if step + MIX_LEAD < TILES:
+                    mix(step + MIX_LEAD, gw)
+            if step == 0:
+                ratio(EARLY_STATS, TILES)
+                make_ln_scale(EARLY_STATS, TILES)
+            if 0 <= step - 3 < TILES and step % 2 == 0:
+                quantize_result((step - 3) // 2)
+            if step - 3 == 2 * EARLY_SCALE_PAIRS - 1:
+                store_scales(nc.sync, early_scales, slice(0, early_docs))
+            for gq in range(QUERY_GROUPS):
+                if 0 <= step - 2 < TILES and not scalar_packs(step - 2, gq):
+                    pack_result(step - 2, gq, False)
             if step < TILES:
-                apply_gain(step, 0)
-            if step >= 1 and step - 1 < TILES and (step == TILES or group_of[step] != group_of[step - 1]):
-                k = group_of[step - 1]
-                quantize_lg(k)
-                banks.extend((k, gq, r) for gq in range(QUERY_GROUPS) for r in range(DOC_GROUPS[k]))
-            if step < TILES:
-                apply_gain(step, 1)
-            for k, gq in to_quantize:
-                quantize_result(k, gq)
-                if gq == QUERY_GROUPS - 1 and k == EARLY_SCALES_GROUP:
-                    store_scales(slice(0, doc_cols(k).stop))
-            to_quantize = to_pack
-            for k, gq in to_pack:
-                pack_result(k, gq)
-            to_pack = []
-            for j, (k, gq, r) in enumerate(banks[:2]):
-                scores(k, gq, r, False)
-                if r == DOC_GROUPS[k] - 1:
-                    store_result(k, gq)
-                    to_pack.append((k, gq))
-            banks = banks[2:]
-            step += 1
-        store_scales(slice(doc_cols(EARLY_SCALES_GROUP).stop, N_DOCS))
+                quantize_lg(step)
+        store_scales(nc.scalar, late_scales, slice(early_docs, N_DOCS))

@@ -29,6 +29,7 @@ MIX_LEAD = 4
 F_SUM_LEAD = 2
 VECTOR_F_SUMS = (9, 11, 13)
 EARLY_STATS = 8
+EARLY_Q_UNITS = 2
 SCALAR_PACKS_BOTH = 3
 SCALAR_PACKS_ONE = 16
 FIRST_Q_STEP = 6
@@ -55,6 +56,8 @@ def tile_paragraphvectorsmoothedqueryloglikelihoo_x2_kernel(
         early_docs = 2 * P * EARLY_SCALE_PAIRS
         early_scales = keep.tile([P, QUERY_GROUPS, early_docs], U8, name="early_scales", align_bytes=64)
         late_scales = keep.tile([P, QUERY_GROUPS, N_DOCS - early_docs], U8, name="late_scales", align_bytes=64)
+        b_cols = keep.tile([P, WORD_PASSES, PACK], BF16, name="b_cols")
+        b_cols_f32 = keep.tile([P, WORD_PASSES, PACK], F32, name="b_cols_f32")
         b_rows = keep.tile([P, N_WORDS], BF16, name="b_rows")
         c_cols = keep.tile([P, WORD_PASSES, PACK], BF16, name="c_cols")
         g_cols = keep.tile([P, WORD_PASSES, PACK], BF16, name="g_cols")
@@ -167,7 +170,7 @@ def tile_paragraphvectorsmoothedqueryloglikelihoo_x2_kernel(
                 cols = slice(BANK * h, BANK * (h + 1))
                 nc.vector.scalar_tensor_tensor(
                     out=by_slot(rows[i][:, cols]), in0=to_slots(z_bank[i, h][:]), scalar=-1.0,
-                    in1=to_slots(b_rows[:, cols]), op0=ALU.mult, op1=ALU.subtract,
+                    in1=by_slot(b_rows[:, cols]), op0=ALU.mult, op1=ALU.subtract,
                 )
 
         def row_max(i):
@@ -292,17 +295,11 @@ def tile_paragraphvectorsmoothedqueryloglikelihoo_x2_kernel(
                         stop=(gw == WORD_PASSES - 1),
                     )
 
-        def store_group(i):
-            return range(i, i + 1) if i >= TILES - 2 else range(i - i % 2, i - i % 2 + 2)
-
-        def result_cols(i, gq):
-            lo = store_group(i).start
-            return result[lo, gq][:, :, P * (i - lo) : P * (i - lo + 1)]
-
         def copy_scores(i, gq):
-            if i == store_group(i).start:
-                result[i, gq] = work.tile([P, PACK, len(store_group(i)) * P], F32, name="result", bufs=6)
-            nc.scalar.copy(out=result_cols(i, gq), in_=score_bank[i, gq][:])
+            result[i, gq] = work.tile([P, PACK, P], F32, name="result", bufs=8)
+            nc.scalar.copy(out=result[i, gq][:], in_=score_bank[i, gq][:])
+            dst = out_0[K_PASS * gq : K_PASS * (gq + 1), P * i : P * (i + 1)].rearrange("(p t) m -> p t m", t=PACK)
+            nc.sync.dma_start(out=dst, in_=result[i, gq][:])
 
         def pack_result(i, gq, on_scalar):
             k, j = divmod(i, 2)
@@ -312,12 +309,10 @@ def tile_paragraphvectorsmoothedqueryloglikelihoo_x2_kernel(
             if on_scalar:
                 nc.scalar.copy(out=dst, in_=score_bank[i, gq][:].rearrange("p t m -> p m t"))
             else:
-                nc.vector.tensor_copy(out=dst, in_=result_cols(i, gq).rearrange("p t m -> p m t"))
-
-        def store_result(tiles, gq):
-            docs = slice(P * tiles.start, P * tiles.stop)
-            dst = out_0[K_PASS * gq : K_PASS * (gq + 1), docs].rearrange("(p t) m -> p t m", t=PACK)
-            nc.sync.dma_start(out=dst, in_=result[tiles.start, gq][:])
+                nc.vector.tensor_copy(
+                    out=dst.rearrange("p (c i) t -> p c t i", i=4),
+                    in_=result[i, gq][:].rearrange("p t (c i) -> p c t i", i=4),
+                )
 
         def quantize_result(k):
             cols = doc_cols(k)
@@ -338,7 +333,7 @@ def tile_paragraphvectorsmoothedqueryloglikelihoo_x2_kernel(
 
         nc.vector.memset(w_scales[:].bitcast(I32), 0)
         nc.vector.memset(warm[:], 0.0)
-        nc.scalar.dma_start(out=b_rows[:], in_=b.partition_broadcast(P))
+        nc.scalar.dma_start(out=b_cols[:], in_=b.rearrange("(w p t) -> p w t", p=P, t=PACK))
         nc.scalar.activation(out=warm[:], in_=warm[:], func=ACT.Exp)
         make_identity(nc, ident[:])
         load_dv(0)
@@ -368,10 +363,17 @@ def tile_paragraphvectorsmoothedqueryloglikelihoo_x2_kernel(
             in1=ident[:, PACK : PACK + 1].unsqueeze(2).to_broadcast([P, PACK, P]),
             op=ALU.add,
         )
+        nc.vector.tensor_copy(out=b_cols_f32[:], in_=b_cols[:])
         transpose_dv(0)
         copy_dv(0)
         quantize_dv(0)
+        for gw in range(WORD_PASSES):
+            b_bank = psum.tile([P, PACK, P], F32, name="b_bank", tag="turn")
+            for t in range(PACK):
+                nc.tensor.transpose(b_bank[:, t, :], b_cols_f32[:, gw, t : t + 1].to_broadcast([P, P]), ident[:])
+            nc.scalar.copy(out=by_slot(b_rows[:, K_PASS * gw : K_PASS * (gw + 1)]), in_=b_bank[:])
         logits(0)
+        logits(1)
         transpose_dv(1)
         copy_dv(1)
         for i in range(F_SUM_LEAD - 1):
@@ -379,16 +381,16 @@ def tile_paragraphvectorsmoothedqueryloglikelihoo_x2_kernel(
         transpose_dv(2)
 
         for i in range(TILES + 1):
+            if i < TILES:
+                add_bias(i)
+            if 2 <= i + 1 < TILES:
+                if i % 2 == 1:
+                    quantize_dv((i + 1) // 2)
+                logits(i + 1)
             if i % 2 == 1 and (i + 5) // 2 < PAIRS:
                 transpose_dv((i + 5) // 2)
             if 0 <= i - FIRST_Q_STEP < 8:
                 transpose_q(i - FIRST_Q_STEP)
-            if i + 1 < TILES:
-                if i % 2 == 1:
-                    quantize_dv((i + 1) // 2)
-                logits(i + 1)
-            if i < TILES:
-                add_bias(i)
             if i % 2 == 0 and (i + 4) // 2 < PAIRS:
                 copy_dv((i + 4) // 2)
             if 0 <= i - FIRST_Q_STEP - 1 < 8:
@@ -398,7 +400,7 @@ def tile_paragraphvectorsmoothedqueryloglikelihoo_x2_kernel(
             if i >= 1:
                 row_max(i - 1)
                 exponentiate(i - 1)
-            if 0 <= i - FIRST_Q_STEP - 4 < 8 and (i - FIRST_Q_STEP - 4) % 2 == 0:
+            if 0 <= i - FIRST_Q_STEP - 4 < 2 * EARLY_Q_UNITS and (i - FIRST_Q_STEP - 4) % 2 == 0:
                 quantize_q((i - FIRST_Q_STEP - 4) // 2)
             c_step(i - 1)
             if i == TILES - 3:
@@ -406,14 +408,15 @@ def tile_paragraphvectorsmoothedqueryloglikelihoo_x2_kernel(
             if i == TILES - 2:
                 ratio(0, EARLY_STATS)
                 make_ln_scale(0, EARLY_STATS)
-            if i == TILES - 1:
-                mix(0, 0)
-                mix(0, 1)
 
+        mix(0, 0)
+        mix(0, 1)
         logarithm(0)
         for i in range(1, MIX_LEAD):
             mix(i, 0)
             mix(i, 1)
+        for unit in range(EARLY_Q_UNITS, 4):
+            quantize_q(unit)
         invert_sums(EARLY_STATS, TILES)
         logarithm(1)
         transpose_log(0)
@@ -426,14 +429,6 @@ def tile_paragraphvectorsmoothedqueryloglikelihoo_x2_kernel(
                 logarithm(step + 2)
             if step + 1 < TILES:
                 transpose_log(step + 1)
-            for gq in range(QUERY_GROUPS):
-                if 0 <= step - 1 < TILES:
-                    scores(step - 1, gq)
-                    copy_scores(step - 1, gq)
-                    if scalar_packs(step - 1, gq):
-                        pack_result(step - 1, gq, True)
-                    if step == store_group(step - 1).stop:
-                        store_result(store_group(step - 1), gq)
             for gw in range(WORD_PASSES):
                 if step < TILES:
                     apply_gain(step, gw)
@@ -446,6 +441,12 @@ def tile_paragraphvectorsmoothedqueryloglikelihoo_x2_kernel(
                 quantize_result((step - 3) // 2)
             if step - 3 == 2 * EARLY_SCALE_PAIRS - 1:
                 store_scales(nc.sync, early_scales, slice(0, early_docs))
+            for gq in range(QUERY_GROUPS):
+                if 0 <= step - 1 < TILES:
+                    scores(step - 1, gq)
+                    copy_scores(step - 1, gq)
+                    if scalar_packs(step - 1, gq):
+                        pack_result(step - 1, gq, True)
             for gq in range(QUERY_GROUPS):
                 if 0 <= step - 2 < TILES and not scalar_packs(step - 2, gq):
                     pack_result(step - 2, gq, False)

@@ -25,13 +25,14 @@ TILES = N_DOCS // P
 PAIRS = TILES // 2
 WORD_PASSES = N_WORDS // K_PASS
 QUERY_GROUPS = N_QUERIES // K_PASS
-MIX_LEAD = 4
+MIX_LEAD = 5
 F_SUM_LEAD = 2
-VECTOR_F_SUMS = (9, 11, 13)
+TENSOR_F_SUMS = 3
+LOG_LEAD = 4
 EARLY_STATS = 8
 EARLY_Q_UNITS = 2
-SCALAR_PACKS_BOTH = 3
-SCALAR_PACKS_ONE = 16
+SCALAR_PACKS_BOTH = 2
+SCALAR_PACKS_ONE = 7
 FIRST_Q_STEP = 6
 EARLY_SCALE_PAIRS = 4
 
@@ -77,7 +78,7 @@ def tile_paragraphvectorsmoothedqueryloglikelihoo_x2_kernel(
         inv_exp_sum, inv_f_sum = inv_sums[:, :, 0], inv_sums[:, :, 1]
         f_ratio = keep.tile([P, TILES], F32, name="f_ratio")
         ln_scale = keep.tile([P, TILES], F32, name="ln_scale")
-        f_copy_v = keep.tile([P, N_WORDS], BF16, name="f_copy_v")
+        ident_bf16 = keep.tile([P, P], BF16, name="ident_bf16")
         f_copy = keep.tile([P, N_WORDS], BF16, name="f_copy")
 
         dv_raw, f_raw, q_raw = {}, {}, {}
@@ -147,8 +148,8 @@ def tile_paragraphvectorsmoothedqueryloglikelihoo_x2_kernel(
         def to_slots(natural):
             return natural.rearrange("p (k t) -> p t k", t=PACK)
 
-        def by_slot(sorted_cols):
-            return sorted_cols.rearrange("p (t k) -> p t k", t=PACK)
+        def pass_of(sorted_row, gw):
+            return sorted_row.rearrange("p (t w k) -> p w t k", t=PACK, w=WORD_PASSES)[:, gw, :, :]
 
         def logits(i):
             docs = slice(P * i, P * (i + 1))
@@ -167,10 +168,9 @@ def tile_paragraphvectorsmoothedqueryloglikelihoo_x2_kernel(
         def add_bias(i):
             rows[i] = keep.tile([P, N_WORDS], F32, name="row%d" % i)
             for h in range(2):
-                cols = slice(BANK * h, BANK * (h + 1))
                 nc.vector.scalar_tensor_tensor(
-                    out=by_slot(rows[i][:, cols]), in0=to_slots(z_bank[i, h][:]), scalar=-1.0,
-                    in1=by_slot(b_rows[:, cols]), op0=ALU.mult, op1=ALU.subtract,
+                    out=pass_of(rows[i][:], h), in0=to_slots(z_bank[i, h][:]), scalar=-1.0,
+                    in1=pass_of(b_rows[:], h), op0=ALU.mult, op1=ALU.subtract,
                 )
 
         def row_max(i):
@@ -186,22 +186,26 @@ def tile_paragraphvectorsmoothedqueryloglikelihoo_x2_kernel(
             return f_raw[i // 2][:, i % 2, :]
 
         def sum_f(i):
-            if i in VECTOR_F_SUMS:
-                nc.vector.tensor_scalar(
-                    out=f_copy_v[:], in0=f_rows(i), scalar1=1.0, scalar2=None, op0=ALU.mult, op1=ALU.add,
-                    accum_out=f_sum[:, i : i + 1],
-                )
-            else:
-                nc.scalar.activation(out=f_copy[:], in_=f_rows(i), func=ACT.Identity, accum_out=f_sum[:, i : i + 1])
+            nc.scalar.activation(out=f_copy[:], in_=f_rows(i), func=ACT.Identity, accum_out=f_sum[:, i : i + 1])
+
+        def sum_f_on_tensor():
+            small_bank["f"] = psum.tile([P, TENSOR_F_SUMS, P], F32, name="f_bank", tag="product")
+            for j in range(TENSOR_F_SUMS):
+                for lo in range(0, N_WORDS, P):
+                    nc.tensor.matmul(
+                        small_bank["f"][:, j, :], lhsT=ident_bf16[:],
+                        rhs=f_rows(TILES - TENSOR_F_SUMS + j)[:, lo : lo + P],
+                        start=(lo == 0), stop=(lo == N_WORDS - P),
+                    )
 
         def ratio(lo, hi):
             nc.vector.tensor_tensor(out=f_ratio[:, lo:hi], in0=exp_sum[:, lo:hi], in1=inv_f_sum[:, lo:hi], op=ALU.mult)
 
-        def mix(i, gw):
-            cols = slice(K_PASS * gw, K_PASS * (gw + 1))
+        def mix(i):
+            by_slot = rows[i][:].rearrange("p (t k) -> p t k", t=PACK)
             nc.vector.scalar_tensor_tensor(
-                out=by_slot(rows[i][:, cols]), in0=to_slots(f_rows(i)[:, cols]), scalar=f_ratio[:, i : i + 1],
-                in1=by_slot(rows[i][:, cols]), op0=ALU.mult, op1=ALU.add,
+                out=by_slot, in0=to_slots(f_rows(i)), scalar=f_ratio[:, i : i + 1], in1=by_slot,
+                op0=ALU.mult, op1=ALU.add,
             )
 
         def invert_sums(lo, hi):
@@ -247,72 +251,94 @@ def tile_paragraphvectorsmoothedqueryloglikelihoo_x2_kernel(
         def logarithm(i):
             nc.scalar.activation(out=rows[i][:], in_=rows[i][:], func=ACT.Ln, scale=ln_scale[:, i : i + 1])
 
-        def transpose_log(i):
-            for gw in range(WORD_PASSES):
+        def transpose_log(k):
+            banks = [(i, gw) for i in (2 * k, 2 * k + 1) for gw in range(WORD_PASSES)]
+            for i, gw in banks:
                 log_bank[i, gw] = psum.tile([P, PACK, P], F32, name="log_bank", tag="turn")
                 nc.tensor.matmul(
                     log_bank[i, gw][:].rearrange("p t n -> p (t n)"), lhsT=shift_rows[:, gw, :],
                     rhs=selector[:].rearrange("p t n -> p (t n)"), start=True, stop=False,
                 )
-            for gw in range(WORD_PASSES):
+            for i, gw in banks:
                 for t in range(PACK):
-                    lo = K_PASS * gw + P * t
                     nc.tensor.matmul(
-                        log_bank[i, gw][:, t, :], lhsT=rows[i][:, lo : lo + P], rhs=ident[:],
+                        log_bank[i, gw][:, t, :], lhsT=pass_of(rows[i][:], gw)[:, t, :], rhs=ident[:],
                         is_transpose=True, start=False, stop=(t == PACK - 1),
                     )
 
-        def apply_gain(i, gw):
-            if gw == 0:
-                lg_packed[i] = work.tile([P, N_WORDS], BF16, name="lg_packed", tag="packed", bufs=6, align_bytes=64)
-            nc.vector.tensor_tensor(
-                out=lg_packed[i][:, BANK * gw : BANK * (gw + 1)].rearrange("p (n t) -> p n t", t=PACK),
-                in0=log_bank[i, gw][:].rearrange("p t n -> p n t"),
-                in1=g_cols[:, gw, :].unsqueeze(1).to_broadcast([P, P, PACK]),
-                op=ALU.mult,
+        def apply_gain(k):
+            lg_packed[k] = work.tile(
+                [P, WORD_PASSES * 2 * BANK], BF16, name="lg_packed", tag="packed", bufs=6, align_bytes=64
             )
+            for j in range(2):
+                for gw in range(WORD_PASSES):
+                    lo = BANK * (2 * gw + j)
+                    nc.vector.tensor_tensor(
+                        out=lg_packed[k][:, lo : lo + BANK].rearrange("p (n t) -> p n t", t=PACK),
+                        in0=log_bank[2 * k + j, gw][:].rearrange("p t n -> p n t"),
+                        in1=g_cols[:, gw, :].unsqueeze(1).to_broadcast([P, P, PACK]),
+                        op=ALU.mult,
+                    )
 
-        def quantize_lg(i):
-            lg_codes[i] = work.tile([P, WORD_PASSES * P], U32, name="lg_codes", bufs=3, align_bytes=64)
-            lg_scales[i] = work.tile([P, WORD_PASSES * P], U8, name="lg_scales", bufs=3, align_bytes=64)
-            nc.vector.quantize_mx(out=lg_codes[i][:].bitcast(FP8X4), scales=lg_scales[i][:], in_=lg_packed[i][:])
+        def quantize_lg(k):
+            lg_codes[k] = work.tile([P, WORD_PASSES * 2 * P], U32, name="lg_codes", bufs=3, align_bytes=64)
+            lg_scales[k] = work.tile([P, WORD_PASSES * 2 * P], U8, name="lg_scales", bufs=3, align_bytes=64)
+            nc.vector.quantize_mx(out=lg_codes[k][:].bitcast(FP8X4), scales=lg_scales[k][:], in_=lg_packed[k][:])
 
         def doc_cols(k):
             return slice(2 * P * k, 2 * P * (k + 1))
 
-        def scores(i, gq):
-            score_bank[i, gq] = psum.tile([P, PACK, P], F32, name="score_bank", tag="product")
-            for t in range(PACK):
-                for gw in range(WORD_PASSES):
-                    lo = K_PASS * (WORD_PASSES * gq + gw) + P * t
-                    nc.tensor.matmul_mx(
-                        out=score_bank[i, gq][:, t, :],
-                        lhsT=q_codes[:, lo : lo + P].bitcast(FP8X4),
-                        lhsT_scale=q_scales[:, lo : lo + P],
-                        rhs=lg_codes[i][:, P * gw : P * (gw + 1)].bitcast(FP8X4),
-                        rhs_scale=lg_scales[i][:, P * gw : P * (gw + 1)],
-                        start=(gw == 0),
-                        stop=(gw == WORD_PASSES - 1),
-                    )
-
-        def copy_scores(i, gq):
-            result[i, gq] = work.tile([P, PACK, P], F32, name="result", bufs=8)
-            nc.scalar.copy(out=result[i, gq][:], in_=score_bank[i, gq][:])
-            dst = out_0[K_PASS * gq : K_PASS * (gq + 1), P * i : P * (i + 1)].rearrange("(p t) m -> p t m", t=PACK)
-            nc.sync.dma_start(out=dst, in_=result[i, gq][:])
-
-        def pack_result(i, gq, on_scalar):
-            k, j = divmod(i, 2)
-            if j == 0:
-                result_packed[k, gq] = work.tile([P, 2 * BANK], BF16, name="result_packed", bufs=4, align_bytes=64)
-            dst = result_packed[k, gq][:, BANK * j : BANK * (j + 1)].rearrange("p (m t) -> p m t", t=PACK)
-            if on_scalar:
-                nc.scalar.copy(out=dst, in_=score_bank[i, gq][:].rearrange("p t m -> p m t"))
-            else:
-                nc.vector.tensor_copy(
-                    out=dst.rearrange("p (c i) t -> p c t i", i=4),
-                    in_=result[i, gq][:].rearrange("p t (c i) -> p c t i", i=4),
+        def score_passes(out, k, gq, t, lo, width):
+            for gw in range(WORD_PASSES):
+                q_cols = slice(K_PASS * (WORD_PASSES * gq + gw) + P * t, K_PASS * (WORD_PASSES * gq + gw) + P * (t + 1))
+                lg_cols = slice(2 * P * gw + lo, 2 * P * gw + lo + width)
+                nc.tensor.matmul_mx(
+                    out=out,
+                    lhsT=q_codes[:, q_cols].bitcast(FP8X4),
+                    lhsT_scale=q_scales[:, q_cols],
+                    rhs=lg_codes[k][:, lg_cols].bitcast(FP8X4),
+                    rhs_scale=lg_scales[k][:, lg_cols],
+                    start=(gw == 0),
+                    stop=(gw == WORD_PASSES - 1),
                 )
+
+        def new_result(k, gq):
+            result[k, gq] = work.tile([P, PACK, 2 * P], F32, name="result", bufs=5)
+            result_packed[k, gq] = work.tile([P, 2 * BANK], BF16, name="result_packed", bufs=4, align_bytes=64)
+
+        def store_result(k, gq):
+            dst = out_0[K_PASS * gq : K_PASS * (gq + 1), doc_cols(k)].rearrange("(p t) m -> p t m", t=PACK)
+            nc.sync.dma_start(out=dst, in_=result[k, gq][:])
+
+        def scores_by_slot(k, gq):
+            new_result(k, gq)
+            for h in range(2):
+                bank = psum.tile([P, 2, 2 * P], F32, name="slot_bank", tag="product")
+                for s in range(2):
+                    score_passes(bank[:, s, :], k, gq, 2 * h + s, 0, 2 * P)
+                nc.scalar.copy(out=result[k, gq][:, 2 * h : 2 * h + 2, :], in_=bank[:])
+            store_result(k, gq)
+
+        def scores_by_tile(k, gq):
+            new_result(k, gq)
+            banks = []
+            for j in range(2):
+                banks.append(psum.tile([P, PACK, P], F32, name="tile_bank", tag="product"))
+                for t in range(PACK):
+                    score_passes(banks[j][:, t, :], k, gq, t, P * j, P)
+                nc.scalar.copy(out=result[k, gq][:, :, P * j : P * (j + 1)], in_=banks[j][:])
+            store_result(k, gq)
+            for j in range(2):
+                nc.scalar.copy(
+                    out=result_packed[k, gq][:, BANK * j : BANK * (j + 1)].rearrange("p (m t) -> p m t", t=PACK),
+                    in_=banks[j][:].rearrange("p t m -> p m t"),
+                )
+
+        def pack_result(k, gq):
+            nc.vector.tensor_copy(
+                out=result_packed[k, gq][:].rearrange("p (c i t) -> p c t i", t=PACK, i=4),
+                in_=result[k, gq][:].rearrange("p t (c i) -> p c t i", i=4),
+            )
 
         def quantize_result(k):
             cols = doc_cols(k)
@@ -343,8 +369,8 @@ def tile_paragraphvectorsmoothedqueryloglikelihoo_x2_kernel(
                 out=w_scales[32 * quad : 32 * quad + 4, :].bitcast(I32),
                 in_=wv_scales[0, 4 * quad : 4 * quad + 4, :].bitcast(I32),
             )
-        load_dv(1)
         load_f(0)
+        load_dv(1)
         load_dv(2)
         load_f(1)
         load_dv(3)
@@ -363,6 +389,7 @@ def tile_paragraphvectorsmoothedqueryloglikelihoo_x2_kernel(
             in1=ident[:, PACK : PACK + 1].unsqueeze(2).to_broadcast([P, PACK, P]),
             op=ALU.add,
         )
+        nc.vector.tensor_copy(out=ident_bf16[:], in_=ident[:])
         nc.vector.tensor_copy(out=b_cols_f32[:], in_=b_cols[:])
         transpose_dv(0)
         copy_dv(0)
@@ -371,12 +398,13 @@ def tile_paragraphvectorsmoothedqueryloglikelihoo_x2_kernel(
             b_bank = psum.tile([P, PACK, P], F32, name="b_bank", tag="turn")
             for t in range(PACK):
                 nc.tensor.transpose(b_bank[:, t, :], b_cols_f32[:, gw, t : t + 1].to_broadcast([P, P]), ident[:])
-            nc.scalar.copy(out=by_slot(b_rows[:, K_PASS * gw : K_PASS * (gw + 1)]), in_=b_bank[:])
+            nc.scalar.copy(out=pass_of(b_rows[:], gw), in_=b_bank[:])
         logits(0)
         logits(1)
         transpose_dv(1)
+        sum_f(0)
         copy_dv(1)
-        for i in range(F_SUM_LEAD - 1):
+        for i in range(1, F_SUM_LEAD - 1):
             sum_f(i)
         transpose_dv(2)
 
@@ -395,7 +423,7 @@ def tile_paragraphvectorsmoothedqueryloglikelihoo_x2_kernel(
                 copy_dv((i + 4) // 2)
             if 0 <= i - FIRST_Q_STEP - 1 < 8:
                 copy_q(i - FIRST_Q_STEP - 1)
-            if i + F_SUM_LEAD - 1 < TILES:
+            if i + F_SUM_LEAD - 1 < TILES - TENSOR_F_SUMS:
                 sum_f(i + F_SUM_LEAD - 1)
             if i >= 1:
                 row_max(i - 1)
@@ -409,47 +437,54 @@ def tile_paragraphvectorsmoothedqueryloglikelihoo_x2_kernel(
                 ratio(0, EARLY_STATS)
                 make_ln_scale(0, EARLY_STATS)
 
-        mix(0, 0)
-        mix(0, 1)
+        mix(0)
         logarithm(0)
+        sum_f_on_tensor()
         for i in range(1, MIX_LEAD):
-            mix(i, 0)
-            mix(i, 1)
+            mix(i)
         for unit in range(EARLY_Q_UNITS, 4):
             quantize_q(unit)
-        invert_sums(EARLY_STATS, TILES)
-        logarithm(1)
+        nc.vector.tensor_reduce(
+            out=f_sum[:, TILES - TENSOR_F_SUMS : TILES], in_=small_bank["f"][:], axis=AX.X, op=ALU.add
+        )
+        for i in range(1, LOG_LEAD):
+            logarithm(i)
         transpose_log(0)
 
-        def scalar_packs(i, gq):
-            return i < SCALAR_PACKS_BOTH or (i < SCALAR_PACKS_ONE and gq == 1)
+        def scalar_packs(k, gq):
+            return k < SCALAR_PACKS_BOTH or (k < SCALAR_PACKS_ONE and gq == 1)
 
-        for step in range(TILES + 4):
-            if step + 2 < TILES:
-                logarithm(step + 2)
-            if step + 1 < TILES:
-                transpose_log(step + 1)
-            for gw in range(WORD_PASSES):
-                if step < TILES:
-                    apply_gain(step, gw)
-                if step + MIX_LEAD < TILES:
-                    mix(step + MIX_LEAD, gw)
-            if step == 0:
+        for k in range(PAIRS + 2):
+            if k < PAIRS:
+                apply_gain(k)
+            if k == 0:
+                invert_sums(EARLY_STATS, TILES)
+            if k == 1:
                 ratio(EARLY_STATS, TILES)
                 make_ln_scale(EARLY_STATS, TILES)
-            if 0 <= step - 3 < TILES and step % 2 == 0:
-                quantize_result((step - 3) // 2)
-            if step - 3 == 2 * EARLY_SCALE_PAIRS - 1:
+            if 2 * k + MIX_LEAD < TILES:
+                mix(2 * k + MIX_LEAD)
+            if 0 <= k - 2:
+                quantize_result(k - 2)
+            if k - 2 == EARLY_SCALE_PAIRS - 1:
                 store_scales(nc.sync, early_scales, slice(0, early_docs))
-            for gq in range(QUERY_GROUPS):
-                if 0 <= step - 1 < TILES:
-                    scores(step - 1, gq)
-                    copy_scores(step - 1, gq)
-                    if scalar_packs(step - 1, gq):
-                        pack_result(step - 1, gq, True)
-            for gq in range(QUERY_GROUPS):
-                if 0 <= step - 2 < TILES and not scalar_packs(step - 2, gq):
-                    pack_result(step - 2, gq, False)
-            if step < TILES:
-                quantize_lg(step)
+            if k < PAIRS:
+                quantize_lg(k)
+            if 2 * k + 1 + MIX_LEAD < TILES:
+                mix(2 * k + 1 + MIX_LEAD)
+            if 0 <= k - 1 < PAIRS:
+                for gq in range(QUERY_GROUPS):
+                    if scalar_packs(k - 1, gq):
+                        scores_by_tile(k - 1, gq)
+                    else:
+                        scores_by_slot(k - 1, gq)
+            for i in (2 * k + LOG_LEAD, 2 * k + 1 + LOG_LEAD):
+                if i < TILES:
+                    logarithm(i)
+            if k + 1 < PAIRS:
+                transpose_log(k + 1)
+            if 0 <= k - 1 < PAIRS:
+                for gq in range(QUERY_GROUPS):
+                    if not scalar_packs(k - 1, gq):
+                        pack_result(k - 1, gq)
         store_scales(nc.scalar, late_scales, slice(early_docs, N_DOCS))

@@ -23,18 +23,30 @@ K_PASS = P * PACK
 BANK = 512
 TILES = N_DOCS // P
 PAIRS = TILES // 2
+PAIR_DOCS = 2 * P
 WORD_PASSES = N_WORDS // K_PASS
 QUERY_GROUPS = N_QUERIES // K_PASS
-MIX_LEAD = 5
-F_SUM_LEAD = 2
-TENSOR_F_SUMS = 3
-LOG_LEAD = 4
-EARLY_STATS = 8
+Q_UNITS = QUERY_GROUPS * WORD_PASSES
+Q_HALVES = 2 * Q_UNITS
+SCALE_QUADS = 4
+LINE = 4
+
+PACKED_BUFS = 6
+RESULT_BUFS = 5
+RESULT_PACKED_BUFS = 4
+CODE_BUFS = 3
+
+FIRST_Q_STEP = TILES - Q_HALVES
 EARLY_Q_UNITS = 2
+FIRST_C_STEP = 2
+EARLY_STATS = TILES // 2
+TENSOR_F_SUMS = 3
+MIX_LEAD = 5
+WARM_AFTER_MIX = 2
+LOG_LEAD = 4
 SCALAR_PACKS_BOTH = 2
 SCALAR_PACKS_ONE = 7
-FIRST_Q_STEP = 6
-EARLY_SCALE_PAIRS = 4
+EARLY_SCALE_PAIRS = PAIRS // 2
 
 
 def tile_paragraphvectorsmoothedqueryloglikelihoo_x2_kernel(
@@ -43,7 +55,7 @@ def tile_paragraphvectorsmoothedqueryloglikelihoo_x2_kernel(
     nc = tc.nc
     with ExitStack() as ctx:
         keep = ctx.enter_context(tc.tile_pool(name="keep", bufs=1))
-        work = ctx.enter_context(tc.tile_pool(name="work", bufs=2))
+        work = ctx.enter_context(tc.tile_pool(name="work", bufs=CODE_BUFS))
         psum = ctx.enter_context(tc.psum_pool(name="psum", bufs=4))
         ctx.enter_context(tc.manual_schedule())
 
@@ -54,7 +66,7 @@ def tile_paragraphvectorsmoothedqueryloglikelihoo_x2_kernel(
         dv_scales = keep.tile([P, N_DOCS], U8, name="dv_scales", align_bytes=64)
         q_codes = keep.tile([P, WORD_PASSES * N_QUERIES], U32, name="q_codes", align_bytes=64)
         q_scales = keep.tile([P, WORD_PASSES * N_QUERIES], U8, name="q_scales", align_bytes=64)
-        early_docs = 2 * P * EARLY_SCALE_PAIRS
+        early_docs = PAIR_DOCS * EARLY_SCALE_PAIRS
         early_scales = keep.tile([P, QUERY_GROUPS, early_docs], U8, name="early_scales", align_bytes=64)
         late_scales = keep.tile([P, QUERY_GROUPS, N_DOCS - early_docs], U8, name="late_scales", align_bytes=64)
         b_cols = keep.tile([P, WORD_PASSES, PACK], BF16, name="b_cols")
@@ -84,26 +96,31 @@ def tile_paragraphvectorsmoothedqueryloglikelihoo_x2_kernel(
         dv_raw, f_raw, q_raw = {}, {}, {}
         dv_bank, dv_packed = {}, {}
         q_bank, q_packed = {}, {}
-        z_bank, rows = {}, {}
-        log_bank, score_bank = {}, {}
+        z_bank, rows, log_bank = {}, {}, {}
         lg_packed, lg_codes, lg_scales = {}, {}, {}
-        result, result_packed = {}, {}
+        result, result_packed, result_codes = {}, {}, {}
         small_bank = {}
+
+        def pair_docs(k):
+            return slice(PAIR_DOCS * k, PAIR_DOCS * (k + 1))
 
         def load_dv(k):
             dv_raw[k] = keep.tile([P, 2, D_MODEL], BF16, name="dv_raw%d" % k)
-            src = dv[2 * P * k : 2 * P * (k + 1), :].rearrange("(j p) d -> p j d", p=P)
+            src = dv[pair_docs(k), :].rearrange("(j p) d -> p j d", p=P)
             nc.sync.dma_start(out=dv_raw[k][:], in_=src)
 
         def load_f(k):
             f_raw[k] = keep.tile([P, 2, N_WORDS], BF16, name="f_raw%d" % k)
-            src = f[2 * P * k : 2 * P * (k + 1), :].rearrange("(j p) v -> p j v", p=P)
+            src = f[pair_docs(k), :].rearrange("(j p) v -> p j v", p=P)
             nc.sync.dma_start(out=f_raw[k][:], in_=src)
 
         def load_q(gq):
             q_raw[gq] = keep.tile([P, PACK, N_WORDS], BF16, name="q_raw%d" % gq)
             src = q[K_PASS * gq : K_PASS * (gq + 1), :].rearrange("(m t) v -> m t v", t=PACK)
             nc.sync.dma_start(out=q_raw[gq][:], in_=src)
+
+        def packed_tile(columns, name):
+            return work.tile([P, columns * PACK], BF16, name=name, tag="packed", bufs=PACKED_BUFS, align_bytes=64)
 
         def transpose_words(bank, sources):
             for j, words in enumerate(sources):
@@ -121,25 +138,26 @@ def tile_paragraphvectorsmoothedqueryloglikelihoo_x2_kernel(
             transpose_words(dv_bank[k], [dv_raw[k][:, j, :].bitcast(F32) for j in range(2)])
 
         def copy_dv(k):
-            dv_packed[k] = work.tile([P, 2 * P * PACK], BF16, name="dv_packed", tag="packed", bufs=6, align_bytes=64)
+            dv_packed[k] = packed_tile(PAIR_DOCS, "dv_packed")
             interleave_words(dv_packed[k][:], dv_bank[k])
 
         def quantize_dv(k):
-            cols = slice(2 * P * k, 2 * P * (k + 1))
+            cols = pair_docs(k)
             nc.vector.quantize_mx(out=dv_codes[:, cols].bitcast(FP8X4), scales=dv_scales[:, cols], in_=dv_packed[k][:])
 
         def transpose_q(h):
             unit, half = divmod(h, 2)
             gq, gw = divmod(unit, WORD_PASSES)
             q_bank[h] = psum.tile([P, 2, 2, P], F32, name="q_bank", tag="turn")
-            words = slice(K_PASS * gw, K_PASS * (gw + 1))
-            transpose_words(q_bank[h], [q_raw[gq][:, 2 * half + j, words].bitcast(F32) for j in range(2)])
+            cols = slice(K_PASS * gw, K_PASS * (gw + 1))
+            transpose_words(q_bank[h], [q_raw[gq][:, 2 * half + j, cols].bitcast(F32) for j in range(2)])
 
         def copy_q(h):
             unit, half = divmod(h, 2)
             if half == 0:
-                q_packed[unit] = work.tile([P, K_PASS * PACK], BF16, name="q_packed", tag="packed", bufs=6, align_bytes=64)
-            interleave_words(q_packed[unit][:, 2 * P * PACK * half : 2 * P * PACK * (half + 1)], q_bank[h])
+                q_packed[unit] = packed_tile(K_PASS, "q_packed")
+            width = 2 * P * PACK
+            interleave_words(q_packed[unit][:, width * half : width * (half + 1)], q_bank[h])
 
         def quantize_q(unit):
             cols = slice(K_PASS * unit, K_PASS * (unit + 1))
@@ -153,24 +171,24 @@ def tile_paragraphvectorsmoothedqueryloglikelihoo_x2_kernel(
 
         def logits(i):
             docs = slice(P * i, P * (i + 1))
-            for h in range(2):
-                z_bank[i, h] = psum.tile([P, BANK], F32, name="z_bank", tag="product")
+            for gw in range(WORD_PASSES):
+                z_bank[i, gw] = psum.tile([P, BANK], F32, name="z_bank", tag="product")
                 nc.tensor.matmul_mx(
-                    out=z_bank[i, h][:],
+                    out=z_bank[i, gw][:],
                     lhsT=dv_codes[:, docs].bitcast(FP8X4),
                     lhsT_scale=dv_scales[:, docs],
-                    rhs=w_codes[:, 2 * BANK * h : 2 * BANK * (h + 1)].bitcast(FP4X4),
-                    rhs_scale=w_scales[:, BANK * h : BANK * (h + 1)],
+                    rhs=w_codes[:, 2 * BANK * gw : 2 * BANK * (gw + 1)].bitcast(FP4X4),
+                    rhs_scale=w_scales[:, BANK * gw : BANK * (gw + 1)],
                     start=True,
                     stop=True,
                 )
 
         def add_bias(i):
             rows[i] = keep.tile([P, N_WORDS], F32, name="row%d" % i)
-            for h in range(2):
+            for gw in range(WORD_PASSES):
                 nc.vector.scalar_tensor_tensor(
-                    out=pass_of(rows[i][:], h), in0=to_slots(z_bank[i, h][:]), scalar=-1.0,
-                    in1=pass_of(b_rows[:], h), op0=ALU.mult, op1=ALU.subtract,
+                    out=pass_of(rows[i][:], gw), in0=to_slots(z_bank[i, gw][:]), scalar=-1.0,
+                    in1=pass_of(b_rows[:], gw), op0=ALU.mult, op1=ALU.subtract,
                 )
 
         def row_max(i):
@@ -223,43 +241,54 @@ def tile_paragraphvectorsmoothedqueryloglikelihoo_x2_kernel(
 
         neg_c = shift_cols[:, :, 0:PACK]
 
-        def c_step(s):
-            if s == 0:
-                nc.vector.tensor_scalar(out=neg_c, in0=c_cols[:], scalar1=-1.0, scalar2=None, op0=ALU.mult)
-            elif s == 1:
-                nc.vector.tensor_reduce(out=c_part[:], in_=neg_c, axis=AX.XY, op=ALU.min)
-                spread("max", c_part[:, 0:1])
-            elif s == 2:
-                nc.vector.tensor_reduce(out=neg_c_max[:], in_=small_bank["max"][:], axis=AX.X, op=ALU.min)
-            elif s == 3:
-                nc.vector.tensor_scalar(
-                    out=shift_cols[:, :, PACK], in0=neg_c_max[:, 0:1].to_broadcast([P, WORD_PASSES]),
-                    scalar1=-1.0, scalar2=None, op0=ALU.mult,
-                )
-                nc.scalar.activation(
-                    out=c_exp[:], in_=neg_c, func=ACT.Exp, scale=-1.0, bias=neg_c_max[:, 0:1], accum_out=c_exp_part[:]
-                )
-            elif s == 4:
-                spread("sum", c_exp_part[:, 0:1])
-                small_bank["rows"] = psum.tile([P, WORD_PASSES, P], F32, name="shift_bank", tag="turn")
-                for gw in range(WORD_PASSES):
-                    nc.tensor.transpose(small_bank["rows"][:, gw, :], shift_cols[:, gw, :], ident[:])
-            elif s == 5:
-                nc.vector.tensor_reduce(out=c_exp_sum[:], in_=small_bank["sum"][:], axis=AX.X, op=ALU.add)
-                nc.scalar.copy(out=shift_rows[:], in_=small_bank["rows"][:])
+        def negate_c():
+            nc.vector.tensor_scalar(out=neg_c, in0=c_cols[:], scalar1=-1.0, scalar2=None, op0=ALU.mult)
+
+        def spread_c_max():
+            nc.vector.tensor_reduce(out=c_part[:], in_=neg_c, axis=AX.XY, op=ALU.min)
+            spread("max", c_part[:, 0:1])
+
+        def finish_c_max():
+            nc.vector.tensor_reduce(out=neg_c_max[:], in_=small_bank["max"][:], axis=AX.X, op=ALU.min)
+
+        def exponentiate_c():
+            nc.vector.tensor_scalar(
+                out=shift_cols[:, :, PACK], in0=neg_c_max[:, 0:1].to_broadcast([P, WORD_PASSES]),
+                scalar1=-1.0, scalar2=None, op0=ALU.mult,
+            )
+            nc.scalar.activation(
+                out=c_exp[:], in_=neg_c, func=ACT.Exp, scale=-1.0, bias=neg_c_max[:, 0:1], accum_out=c_exp_part[:]
+            )
+
+        def spread_c_sum():
+            spread("sum", c_exp_part[:, 0:1])
+            small_bank["rows"] = psum.tile([P, WORD_PASSES, P], F32, name="shift_bank", tag="turn")
+            for gw in range(WORD_PASSES):
+                nc.tensor.transpose(small_bank["rows"][:, gw, :], shift_cols[:, gw, :], ident[:])
+
+        def finish_c_sum():
+            nc.vector.tensor_reduce(out=c_exp_sum[:], in_=small_bank["sum"][:], axis=AX.X, op=ALU.add)
+            nc.scalar.copy(out=shift_rows[:], in_=small_bank["rows"][:])
+
+        c_links = [negate_c, spread_c_max, finish_c_max, exponentiate_c, None, spread_c_sum, finish_c_sum]
+        c_chain = {FIRST_C_STEP + n: link for n, link in enumerate(c_links) if link is not None}
 
         def logarithm(i):
             nc.scalar.activation(out=rows[i][:], in_=rows[i][:], func=ACT.Ln, scale=ln_scale[:, i : i + 1])
 
-        def transpose_log(k):
-            banks = [(i, gw) for i in (2 * k, 2 * k + 1) for gw in range(WORD_PASSES)]
-            for i, gw in banks:
+        def log_banks(k):
+            return [(i, gw) for i in (2 * k, 2 * k + 1) for gw in range(WORD_PASSES)]
+
+        def lay_shift(k):
+            for i, gw in log_banks(k):
                 log_bank[i, gw] = psum.tile([P, PACK, P], F32, name="log_bank", tag="turn")
                 nc.tensor.matmul(
                     log_bank[i, gw][:].rearrange("p t n -> p (t n)"), lhsT=shift_rows[:, gw, :],
                     rhs=selector[:].rearrange("p t n -> p (t n)"), start=True, stop=False,
                 )
-            for i, gw in banks:
+
+        def transpose_log(k):
+            for i, gw in log_banks(k):
                 for t in range(PACK):
                     nc.tensor.matmul(
                         log_bank[i, gw][:, t, :], lhsT=pass_of(rows[i][:], gw)[:, t, :], rhs=ident[:],
@@ -267,9 +296,7 @@ def tile_paragraphvectorsmoothedqueryloglikelihoo_x2_kernel(
                     )
 
         def apply_gain(k):
-            lg_packed[k] = work.tile(
-                [P, WORD_PASSES * 2 * BANK], BF16, name="lg_packed", tag="packed", bufs=6, align_bytes=64
-            )
+            lg_packed[k] = packed_tile(WORD_PASSES * PAIR_DOCS, "lg_packed")
             for j in range(2):
                 for gw in range(WORD_PASSES):
                     lo = BANK * (2 * gw + j)
@@ -281,17 +308,15 @@ def tile_paragraphvectorsmoothedqueryloglikelihoo_x2_kernel(
                     )
 
         def quantize_lg(k):
-            lg_codes[k] = work.tile([P, WORD_PASSES * 2 * P], U32, name="lg_codes", bufs=3, align_bytes=64)
-            lg_scales[k] = work.tile([P, WORD_PASSES * 2 * P], U8, name="lg_scales", bufs=3, align_bytes=64)
+            lg_codes[k] = work.tile([P, WORD_PASSES * PAIR_DOCS], U32, name="lg_codes", align_bytes=64)
+            lg_scales[k] = work.tile([P, WORD_PASSES * PAIR_DOCS], U8, name="lg_scales", align_bytes=64)
             nc.vector.quantize_mx(out=lg_codes[k][:].bitcast(FP8X4), scales=lg_scales[k][:], in_=lg_packed[k][:])
-
-        def doc_cols(k):
-            return slice(2 * P * k, 2 * P * (k + 1))
 
         def score_passes(out, k, gq, t, lo, width):
             for gw in range(WORD_PASSES):
-                q_cols = slice(K_PASS * (WORD_PASSES * gq + gw) + P * t, K_PASS * (WORD_PASSES * gq + gw) + P * (t + 1))
-                lg_cols = slice(2 * P * gw + lo, 2 * P * gw + lo + width)
+                first = K_PASS * (WORD_PASSES * gq + gw) + P * t
+                q_cols = slice(first, first + P)
+                lg_cols = slice(PAIR_DOCS * gw + lo, PAIR_DOCS * gw + lo + width)
                 nc.tensor.matmul_mx(
                     out=out,
                     lhsT=q_codes[:, q_cols].bitcast(FP8X4),
@@ -303,20 +328,22 @@ def tile_paragraphvectorsmoothedqueryloglikelihoo_x2_kernel(
                 )
 
         def new_result(k, gq):
-            result[k, gq] = work.tile([P, PACK, 2 * P], F32, name="result", bufs=5)
-            result_packed[k, gq] = work.tile([P, 2 * BANK], BF16, name="result_packed", bufs=4, align_bytes=64)
+            result[k, gq] = work.tile([P, PACK, PAIR_DOCS], F32, name="result", bufs=RESULT_BUFS)
+            result_packed[k, gq] = work.tile(
+                [P, PAIR_DOCS * PACK], BF16, name="result_packed", bufs=RESULT_PACKED_BUFS, align_bytes=64
+            )
 
         def store_result(k, gq):
-            dst = out_0[K_PASS * gq : K_PASS * (gq + 1), doc_cols(k)].rearrange("(p t) m -> p t m", t=PACK)
+            dst = out_0[K_PASS * gq : K_PASS * (gq + 1), pair_docs(k)].rearrange("(p t) m -> p t m", t=PACK)
             nc.sync.dma_start(out=dst, in_=result[k, gq][:])
 
         def scores_by_slot(k, gq):
             new_result(k, gq)
-            for h in range(2):
-                bank = psum.tile([P, 2, 2 * P], F32, name="slot_bank", tag="product")
+            for t0 in range(0, PACK, 2):
+                bank = psum.tile([P, 2, PAIR_DOCS], F32, name="slot_bank", tag="product")
                 for s in range(2):
-                    score_passes(bank[:, s, :], k, gq, 2 * h + s, 0, 2 * P)
-                nc.scalar.copy(out=result[k, gq][:, 2 * h : 2 * h + 2, :], in_=bank[:])
+                    score_passes(bank[:, s, :], k, gq, t0 + s, 0, PAIR_DOCS)
+                nc.scalar.copy(out=result[k, gq][:, t0 : t0 + 2, :], in_=bank[:])
             store_result(k, gq)
 
         def scores_by_tile(k, gq):
@@ -336,24 +363,28 @@ def tile_paragraphvectorsmoothedqueryloglikelihoo_x2_kernel(
 
         def pack_result(k, gq):
             nc.vector.tensor_copy(
-                out=result_packed[k, gq][:].rearrange("p (c i t) -> p c t i", t=PACK, i=4),
-                in_=result[k, gq][:].rearrange("p t (c i) -> p c t i", i=4),
+                out=result_packed[k, gq][:].rearrange("p (c i t) -> p c t i", t=PACK, i=LINE),
+                in_=result[k, gq][:].rearrange("p t (c i) -> p c t i", i=LINE),
             )
 
         def quantize_result(k):
-            cols = doc_cols(k)
-            codes = work.tile([P, QUERY_GROUPS, 2 * P], U32, name="result_codes", bufs=3, align_bytes=64)
+            cols = pair_docs(k)
+            result_codes[k] = work.tile([P, QUERY_GROUPS, PAIR_DOCS], U32, name="result_codes", align_bytes=64)
             for gq in range(QUERY_GROUPS):
                 if k < EARLY_SCALE_PAIRS:
                     scales = early_scales[:, gq, cols]
                 else:
                     scales = late_scales[:, gq, cols.start - early_docs : cols.stop - early_docs]
-                nc.vector.quantize_mx(out=codes[:, gq, :].bitcast(FP8X4), scales=scales, in_=result_packed[k, gq][:])
-            dst = out_1[:, :, cols, :].rearrange("g p m t -> p g (m t)").bitcast(I32)
-            nc.sync.dma_start(out=dst, in_=codes[:].bitcast(I32))
+                nc.vector.quantize_mx(
+                    out=result_codes[k][:, gq, :].bitcast(FP8X4), scales=scales, in_=result_packed[k, gq][:]
+                )
+
+        def store_codes(k):
+            dst = out_1[:, :, pair_docs(k), :].rearrange("g p m t -> p g (m t)").bitcast(I32)
+            nc.sync.dma_start(out=dst, in_=result_codes[k][:].bitcast(I32))
 
         def store_scales(queue, scales, cols):
-            for quad in range(4):
+            for quad in range(SCALE_QUADS):
                 dst = out_2[:, 4 * quad : 4 * quad + 4, cols].rearrange("g r m -> r g m").bitcast(I32)
                 queue.dma_start(out=dst, in_=scales[32 * quad : 32 * quad + 4, :, :].bitcast(I32))
 
@@ -364,24 +395,26 @@ def tile_paragraphvectorsmoothedqueryloglikelihoo_x2_kernel(
         make_identity(nc, ident[:])
         load_dv(0)
         nc.sync.dma_start(out=w_codes[:].bitcast(I32), in_=wv_words[0].bitcast(I32))
-        for quad in range(4):
+        for quad in range(SCALE_QUADS):
             nc.sync.dma_start(
                 out=w_scales[32 * quad : 32 * quad + 4, :].bitcast(I32),
                 in_=wv_scales[0, 4 * quad : 4 * quad + 4, :].bitcast(I32),
             )
-        load_f(0)
         load_dv(1)
+        load_f(0)
         load_dv(2)
         load_f(1)
         load_dv(3)
         nc.sync.dma_start(out=c_cols[:], in_=c.rearrange("(w p t) -> p w t", p=P, t=PACK))
         nc.sync.dma_start(out=g_cols[:], in_=g.rearrange("(w p t) -> p w t", p=P, t=PACK))
+        q_load_after = (3, 5)
         for k in range(2, PAIRS):
             load_f(k)
             if k + 2 < PAIRS:
                 load_dv(k + 2)
-            if k in (3, 5):
-                load_q(k // 2 - 1)
+            if k in q_load_after:
+                load_q(q_load_after.index(k))
+
         nc.vector.memset(shift_cols[:], 0.0)
         nc.vector.tensor_tensor(
             out=selector[:],
@@ -389,7 +422,6 @@ def tile_paragraphvectorsmoothedqueryloglikelihoo_x2_kernel(
             in1=ident[:, PACK : PACK + 1].unsqueeze(2).to_broadcast([P, PACK, P]),
             op=ALU.add,
         )
-        nc.vector.tensor_copy(out=ident_bf16[:], in_=ident[:])
         nc.vector.tensor_copy(out=b_cols_f32[:], in_=b_cols[:])
         transpose_dv(0)
         copy_dv(0)
@@ -400,37 +432,44 @@ def tile_paragraphvectorsmoothedqueryloglikelihoo_x2_kernel(
                 nc.tensor.transpose(b_bank[:, t, :], b_cols_f32[:, gw, t : t + 1].to_broadcast([P, P]), ident[:])
             nc.scalar.copy(out=pass_of(b_rows[:], gw), in_=b_bank[:])
         logits(0)
-        logits(1)
         transpose_dv(1)
+        logits(1)
         sum_f(0)
         copy_dv(1)
-        for i in range(1, F_SUM_LEAD - 1):
-            sum_f(i)
-        transpose_dv(2)
+        add_bias(0)
+        sum_f(1)
+        row_max(0)
+        exponentiate(0)
+        quantize_dv(1)
 
-        for i in range(TILES + 1):
+        for i in range(1, TILES + 1):
+            h = i - FIRST_Q_STEP
             if i < TILES:
                 add_bias(i)
-            if 2 <= i + 1 < TILES:
-                if i % 2 == 1:
-                    quantize_dv((i + 1) // 2)
+            if i + 1 < TILES:
+                if i % 2 == 0 and i // 2 + 1 < PAIRS:
+                    quantize_dv(i // 2 + 1)
                 logits(i + 1)
+            if i == 1:
+                transpose_dv(2)
+                copy_dv(2)
             if i % 2 == 1 and (i + 5) // 2 < PAIRS:
                 transpose_dv((i + 5) // 2)
-            if 0 <= i - FIRST_Q_STEP < 8:
-                transpose_q(i - FIRST_Q_STEP)
+            if 0 <= h < Q_HALVES:
+                transpose_q(h)
             if i % 2 == 0 and (i + 4) // 2 < PAIRS:
                 copy_dv((i + 4) // 2)
-            if 0 <= i - FIRST_Q_STEP - 1 < 8:
-                copy_q(i - FIRST_Q_STEP - 1)
-            if i + F_SUM_LEAD - 1 < TILES - TENSOR_F_SUMS:
-                sum_f(i + F_SUM_LEAD - 1)
-            if i >= 1:
+            if 0 <= h - 1 < Q_HALVES:
+                copy_q(h - 1)
+            if i + 1 < TILES - TENSOR_F_SUMS:
+                sum_f(i + 1)
+            if i >= 2:
                 row_max(i - 1)
                 exponentiate(i - 1)
-            if 0 <= i - FIRST_Q_STEP - 4 < 2 * EARLY_Q_UNITS and (i - FIRST_Q_STEP - 4) % 2 == 0:
-                quantize_q((i - FIRST_Q_STEP - 4) // 2)
-            c_step(i - 1)
+            if h % 2 == 0 and 0 <= h // 2 - 2 < EARLY_Q_UNITS:
+                quantize_q(h // 2 - 2)
+            if i in c_chain:
+                c_chain[i]()
             if i == TILES - 3:
                 invert_sums(0, EARLY_STATS)
             if i == TILES - 2:
@@ -439,10 +478,13 @@ def tile_paragraphvectorsmoothedqueryloglikelihoo_x2_kernel(
 
         mix(0)
         logarithm(0)
-        sum_f_on_tensor()
+        lay_shift(0)
         for i in range(1, MIX_LEAD):
             mix(i)
-        for unit in range(EARLY_Q_UNITS, 4):
+            if i == WARM_AFTER_MIX:
+                nc.vector.tensor_copy(out=ident_bf16[:], in_=ident[:])
+                sum_f_on_tensor()
+        for unit in range(EARLY_Q_UNITS, Q_UNITS):
             quantize_q(unit)
         nc.vector.tensor_reduce(
             out=f_sum[:, TILES - TENSOR_F_SUMS : TILES], in_=small_bank["f"][:], axis=AX.X, op=ALU.add
@@ -457,19 +499,17 @@ def tile_paragraphvectorsmoothedqueryloglikelihoo_x2_kernel(
         for k in range(PAIRS + 2):
             if k < PAIRS:
                 apply_gain(k)
-            if k == 0:
-                invert_sums(EARLY_STATS, TILES)
             if k == 1:
                 ratio(EARLY_STATS, TILES)
                 make_ln_scale(EARLY_STATS, TILES)
             if 2 * k + MIX_LEAD < TILES:
                 mix(2 * k + MIX_LEAD)
-            if 0 <= k - 2:
-                quantize_result(k - 2)
-            if k - 2 == EARLY_SCALE_PAIRS - 1:
-                store_scales(nc.sync, early_scales, slice(0, early_docs))
             if k < PAIRS:
                 quantize_lg(k)
+            if 0 <= k - 2:
+                quantize_result(k - 2)
+            if k == 0:
+                invert_sums(EARLY_STATS, TILES)
             if 2 * k + 1 + MIX_LEAD < TILES:
                 mix(2 * k + 1 + MIX_LEAD)
             if 0 <= k - 1 < PAIRS:
@@ -478,10 +518,15 @@ def tile_paragraphvectorsmoothedqueryloglikelihoo_x2_kernel(
                         scores_by_tile(k - 1, gq)
                     else:
                         scores_by_slot(k - 1, gq)
+            if 0 <= k - 2:
+                store_codes(k - 2)
+            if k - 2 == EARLY_SCALE_PAIRS - 1:
+                store_scales(nc.sync, early_scales, slice(0, early_docs))
             for i in (2 * k + LOG_LEAD, 2 * k + 1 + LOG_LEAD):
                 if i < TILES:
                     logarithm(i)
             if k + 1 < PAIRS:
+                lay_shift(k + 1)
                 transpose_log(k + 1)
             if 0 <= k - 1 < PAIRS:
                 for gq in range(QUERY_GROUPS):

from contextlib import ExitStack

import concourse.mybir as mybir
from concourse.masks import make_identity

N_DOCS, N_WORDS, D_MODEL, N_QUERIES = 2048, 1024, 512, 1024
FLOPS = 2 * N_DOCS * D_MODEL * N_WORDS + 2 * N_QUERIES * N_WORDS * N_DOCS

F32 = mybir.dt.float32
BF16 = mybir.dt.bfloat16
I32 = mybir.dt.int32
U32 = mybir.dt.uint32
U8 = mybir.dt.uint8
FP8X4 = mybir.dt.float8_e4m3fn_x4
FP4X4 = mybir.dt.float4_e2m1fn_x4
ACT = mybir.ActivationFunctionType
ALU = mybir.AluOpType
AX = mybir.AxisListType

P = 128
PACK = 4
K_PASS = P * PACK
BANK = 512
TILES = N_DOCS // P
PAIRS = TILES // 2
PAIR_DOCS = 2 * P
WORD_PASSES = N_WORDS // K_PASS
QUERY_GROUPS = N_QUERIES // K_PASS
Q_UNITS = QUERY_GROUPS * WORD_PASSES
Q_HALVES = 2 * Q_UNITS
SCALE_QUADS = 4
LINE = 4

PACKED_BUFS = 6
RESULT_BUFS = 5
RESULT_PACKED_BUFS = 4
CODE_BUFS = 3

FIRST_Q_STEP = TILES - Q_HALVES
EARLY_Q_UNITS = 2
FIRST_C_STEP = 2
EARLY_STATS = TILES // 2
TENSOR_F_SUMS = 3
MIX_LEAD = 5
WARM_AFTER_MIX = 2
LOG_LEAD = 4
SCALAR_PACKS_BOTH = 2
SCALAR_PACKS_ONE = 7
EARLY_SCALE_PAIRS = PAIRS // 2


def tile_paragraphvectorsmoothedqueryloglikelihoo_x2_kernel(
    tc, dv, wv_words, wv_scales, b, f, c, g, q, out_0, out_1, out_2
):
    nc = tc.nc
    with ExitStack() as ctx:
        keep = ctx.enter_context(tc.tile_pool(name="keep", bufs=1))
        work = ctx.enter_context(tc.tile_pool(name="work", bufs=CODE_BUFS))
        psum = ctx.enter_context(tc.psum_pool(name="psum", bufs=4))
        ctx.enter_context(tc.manual_schedule())

        ident = keep.tile([P, P], F32, name="ident")
        w_codes = keep.tile([P, 2 * N_WORDS], U8, name="w_codes", align_bytes=64)
        w_scales = keep.tile([P, N_WORDS], U8, name="w_scales", align_bytes=64)
        dv_codes = keep.tile([P, N_DOCS], U32, name="dv_codes", align_bytes=64)
        dv_scales = keep.tile([P, N_DOCS], U8, name="dv_scales", align_bytes=64)
        q_codes = keep.tile([P, WORD_PASSES * N_QUERIES], U32, name="q_codes", align_bytes=64)
        q_scales = keep.tile([P, WORD_PASSES * N_QUERIES], U8, name="q_scales", align_bytes=64)
        early_docs = PAIR_DOCS * EARLY_SCALE_PAIRS
        early_scales = keep.tile([P, QUERY_GROUPS, early_docs], U8, name="early_scales", align_bytes=64)
        late_scales = keep.tile([P, QUERY_GROUPS, N_DOCS - early_docs], U8, name="late_scales", align_bytes=64)
        b_cols = keep.tile([P, WORD_PASSES, PACK], BF16, name="b_cols")
        b_cols_f32 = keep.tile([P, WORD_PASSES, PACK], F32, name="b_cols_f32")
        b_rows = keep.tile([P, N_WORDS], BF16, name="b_rows")
        c_cols = keep.tile([P, WORD_PASSES, PACK], BF16, name="c_cols")
        g_cols = keep.tile([P, WORD_PASSES, PACK], BF16, name="g_cols")
        shift_cols = keep.tile([P, WORD_PASSES, P], F32, name="shift_cols")
        shift_rows = keep.tile([P, WORD_PASSES, P], BF16, name="shift_rows")
        selector = keep.tile([P, PACK, P], BF16, name="selector")
        warm = keep.tile([P, 1], F32, name="warm")
        c_part = keep.tile([P, 1], F32, name="c_part")
        neg_c_max = keep.tile([P, 1], F32, name="neg_c_max")
        c_exp = keep.tile([P, WORD_PASSES, PACK], F32, name="c_exp")
        c_exp_part = keep.tile([P, 1], F32, name="c_exp_part")
        c_exp_sum = keep.tile([P, 1], F32, name="c_exp_sum")
        neg_max = keep.tile([P, TILES], F32, name="neg_max")
        sums = keep.tile([P, TILES, 2], F32, name="sums")
        inv_sums = keep.tile([P, TILES, 2], F32, name="inv_sums")
        exp_sum, f_sum = sums[:, :, 0], sums[:, :, 1]
        inv_exp_sum, inv_f_sum = inv_sums[:, :, 0], inv_sums[:, :, 1]
        f_ratio = keep.tile([P, TILES], F32, name="f_ratio")
        ln_scale = keep.tile([P, TILES], F32, name="ln_scale")
        ident_bf16 = keep.tile([P, P], BF16, name="ident_bf16")
        f_copy = keep.tile([P, N_WORDS], BF16, name="f_copy")

        dv_raw, f_raw, q_raw = {}, {}, {}
        dv_bank, dv_packed = {}, {}
        q_bank, q_packed = {}, {}
        z_bank, rows, log_bank = {}, {}, {}
        lg_packed, lg_codes, lg_scales = {}, {}, {}
        result, result_packed, result_codes = {}, {}, {}
        small_bank = {}

        def pair_docs(k):
            return slice(PAIR_DOCS * k, PAIR_DOCS * (k + 1))

        def load_dv(k):
            dv_raw[k] = keep.tile([P, 2, D_MODEL], BF16, name="dv_raw%d" % k)
            src = dv[pair_docs(k), :].rearrange("(j p) d -> p j d", p=P)
            nc.sync.dma_start(out=dv_raw[k][:], in_=src)

        def load_f(k):
            f_raw[k] = keep.tile([P, 2, N_WORDS], BF16, name="f_raw%d" % k)
            src = f[pair_docs(k), :].rearrange("(j p) v -> p j v", p=P)
            nc.sync.dma_start(out=f_raw[k][:], in_=src)

        def load_q(gq):
            q_raw[gq] = keep.tile([P, PACK, N_WORDS], BF16, name="q_raw%d" % gq)
            src = q[K_PASS * gq : K_PASS * (gq + 1), :].rearrange("(m t) v -> m t v", t=PACK)
            nc.sync.dma_start(out=q_raw[gq][:], in_=src)

        def packed_tile(columns, name):
            return work.tile([P, columns * PACK], BF16, name=name, tag="packed", bufs=PACKED_BUFS, align_bytes=64)

        def transpose_words(bank, sources):
            for j, words in enumerate(sources):
                for u in range(2):
                    nc.tensor.transpose(bank[:, j, u, :], words[:, u : 2 * P : 2], ident[:])

        def interleave_words(packed_cols, bank):
            nc.scalar.copy(
                out=packed_cols.bitcast(F32).rearrange("p (j r u) -> p j r u", j=2, u=2),
                in_=bank[:].rearrange("p j u r -> p j r u"),
            )

        def transpose_dv(k):
            dv_bank[k] = psum.tile([P, 2, 2, P], F32, name="dv_bank", tag="turn")
            transpose_words(dv_bank[k], [dv_raw[k][:, j, :].bitcast(F32) for j in range(2)])

        def copy_dv(k):
            dv_packed[k] = packed_tile(PAIR_DOCS, "dv_packed")
            interleave_words(dv_packed[k][:], dv_bank[k])

        def quantize_dv(k):
            cols = pair_docs(k)
            nc.vector.quantize_mx(out=dv_codes[:, cols].bitcast(FP8X4), scales=dv_scales[:, cols], in_=dv_packed[k][:])

        def transpose_q(h):
            unit, half = divmod(h, 2)
            gq, gw = divmod(unit, WORD_PASSES)
            q_bank[h] = psum.tile([P, 2, 2, P], F32, name="q_bank", tag="turn")
            cols = slice(K_PASS * gw, K_PASS * (gw + 1))
            transpose_words(q_bank[h], [q_raw[gq][:, 2 * half + j, cols].bitcast(F32) for j in range(2)])

        def copy_q(h):
            unit, half = divmod(h, 2)
            if half == 0:
                q_packed[unit] = packed_tile(K_PASS, "q_packed")
            width = 2 * P * PACK
            interleave_words(q_packed[unit][:, width * half : width * (half + 1)], q_bank[h])

        def quantize_q(unit):
            cols = slice(K_PASS * unit, K_PASS * (unit + 1))
            nc.vector.quantize_mx(out=q_codes[:, cols].bitcast(FP8X4), scales=q_scales[:, cols], in_=q_packed[unit][:])

        def to_slots(natural):
            return natural.rearrange("p (k t) -> p t k", t=PACK)

        def pass_of(sorted_row, gw):
            return sorted_row.rearrange("p (t w k) -> p w t k", t=PACK, w=WORD_PASSES)[:, gw, :, :]

        def logits(i):
            docs = slice(P * i, P * (i + 1))
            for gw in range(WORD_PASSES):
                z_bank[i, gw] = psum.tile([P, BANK], F32, name="z_bank", tag="product")
                nc.tensor.matmul_mx(
                    out=z_bank[i, gw][:],
                    lhsT=dv_codes[:, docs].bitcast(FP8X4),
                    lhsT_scale=dv_scales[:, docs],
                    rhs=w_codes[:, 2 * BANK * gw : 2 * BANK * (gw + 1)].bitcast(FP4X4),
                    rhs_scale=w_scales[:, BANK * gw : BANK * (gw + 1)],
                    start=True,
                    stop=True,
                )

        def add_bias(i):
            rows[i] = keep.tile([P, N_WORDS], F32, name="row%d" % i)
            for gw in range(WORD_PASSES):
                nc.vector.scalar_tensor_tensor(
                    out=pass_of(rows[i][:], gw), in0=to_slots(z_bank[i, gw][:]), scalar=-1.0,
                    in1=pass_of(b_rows[:], gw), op0=ALU.mult, op1=ALU.subtract,
                )

        def row_max(i):
            nc.vector.tensor_reduce(out=neg_max[:, i : i + 1], in_=rows[i][:], axis=AX.X, op=ALU.min)

        def exponentiate(i):
            nc.scalar.activation(
                out=rows[i][:], in_=rows[i][:], func=ACT.Exp, scale=-1.0, bias=neg_max[:, i : i + 1],
                accum_out=exp_sum[:, i : i + 1],
            )

        def f_rows(i):
            return f_raw[i // 2][:, i % 2, :]

        def sum_f(i):
            nc.scalar.activation(out=f_copy[:], in_=f_rows(i), func=ACT.Identity, accum_out=f_sum[:, i : i + 1])

        def sum_f_on_tensor():
            small_bank["f"] = psum.tile([P, TENSOR_F_SUMS, P], F32, name="f_bank", tag="product")
            for j in range(TENSOR_F_SUMS):
                for lo in range(0, N_WORDS, P):
                    nc.tensor.matmul(
                        small_bank["f"][:, j, :], lhsT=ident_bf16[:],
                        rhs=f_rows(TILES - TENSOR_F_SUMS + j)[:, lo : lo + P],
                        start=(lo == 0), stop=(lo == N_WORDS - P),
                    )

        def ratio(lo, hi):
            nc.vector.tensor_tensor(out=f_ratio[:, lo:hi], in0=exp_sum[:, lo:hi], in1=inv_f_sum[:, lo:hi], op=ALU.mult)

        def mix(i):
            by_slot = rows[i][:].rearrange("p (t k) -> p t k", t=PACK)
            nc.vector.scalar_tensor_tensor(
                out=by_slot, in0=to_slots(f_rows(i)), scalar=f_ratio[:, i : i + 1], in1=by_slot,
                op0=ALU.mult, op1=ALU.add,
            )

        def invert_sums(lo, hi):
            nc.vector.reciprocal(out=inv_sums[:, lo:hi, :], in_=sums[:, lo:hi, :])

        def make_ln_scale(lo, hi):
            nc.vector.tensor_scalar(
                out=ln_scale[:, lo:hi], in0=inv_exp_sum[:, lo:hi], scalar1=c_exp_sum[:, 0:1], scalar2=0.5,
                op0=ALU.mult, op1=ALU.mult,
            )

        def spread(name, column):
            small_bank[name] = psum.tile([P, P], F32, name="spread_bank", tag="turn")
            nc.tensor.transpose(small_bank[name][:], column.to_broadcast([P, P]), ident[:])

        neg_c = shift_cols[:, :, 0:PACK]

        def negate_c():
            nc.vector.tensor_scalar(out=neg_c, in0=c_cols[:], scalar1=-1.0, scalar2=None, op0=ALU.mult)

        def spread_c_max():
            nc.vector.tensor_reduce(out=c_part[:], in_=neg_c, axis=AX.XY, op=ALU.min)
            spread("max", c_part[:, 0:1])

        def finish_c_max():
            nc.vector.tensor_reduce(out=neg_c_max[:], in_=small_bank["max"][:], axis=AX.X, op=ALU.min)

        def exponentiate_c():
            nc.vector.tensor_scalar(
                out=shift_cols[:, :, PACK], in0=neg_c_max[:, 0:1].to_broadcast([P, WORD_PASSES]),
                scalar1=-1.0, scalar2=None, op0=ALU.mult,
            )
            nc.scalar.activation(
                out=c_exp[:], in_=neg_c, func=ACT.Exp, scale=-1.0, bias=neg_c_max[:, 0:1], accum_out=c_exp_part[:]
            )

        def spread_c_sum():
            spread("sum", c_exp_part[:, 0:1])
            small_bank["rows"] = psum.tile([P, WORD_PASSES, P], F32, name="shift_bank", tag="turn")
            for gw in range(WORD_PASSES):
                nc.tensor.transpose(small_bank["rows"][:, gw, :], shift_cols[:, gw, :], ident[:])

        def finish_c_sum():
            nc.vector.tensor_reduce(out=c_exp_sum[:], in_=small_bank["sum"][:], axis=AX.X, op=ALU.add)
            nc.scalar.copy(out=shift_rows[:], in_=small_bank["rows"][:])

        c_links = [negate_c, spread_c_max, finish_c_max, exponentiate_c, None, spread_c_sum, finish_c_sum]
        c_chain = {FIRST_C_STEP + n: link for n, link in enumerate(c_links) if link is not None}

        def logarithm(i):
            nc.scalar.activation(out=rows[i][:], in_=rows[i][:], func=ACT.Ln, scale=ln_scale[:, i : i + 1])

        def log_banks(k):
            return [(i, gw) for i in (2 * k, 2 * k + 1) for gw in range(WORD_PASSES)]

        def lay_shift(k):
            for i, gw in log_banks(k):
                log_bank[i, gw] = psum.tile([P, PACK, P], F32, name="log_bank", tag="turn")
                nc.tensor.matmul(
                    log_bank[i, gw][:].rearrange("p t n -> p (t n)"), lhsT=shift_rows[:, gw, :],
                    rhs=selector[:].rearrange("p t n -> p (t n)"), start=True, stop=False,
                )

        def transpose_log(k):
            for i, gw in log_banks(k):
                for t in range(PACK):
                    nc.tensor.matmul(
                        log_bank[i, gw][:, t, :], lhsT=pass_of(rows[i][:], gw)[:, t, :], rhs=ident[:],
                        is_transpose=True, start=False, stop=(t == PACK - 1),
                    )

        def apply_gain(k):
            lg_packed[k] = packed_tile(WORD_PASSES * PAIR_DOCS, "lg_packed")
            for j in range(2):
                for gw in range(WORD_PASSES):
                    lo = BANK * (2 * gw + j)
                    nc.vector.tensor_tensor(
                        out=lg_packed[k][:, lo : lo + BANK].rearrange("p (n t) -> p n t", t=PACK),
                        in0=log_bank[2 * k + j, gw][:].rearrange("p t n -> p n t"),
                        in1=g_cols[:, gw, :].unsqueeze(1).to_broadcast([P, P, PACK]),
                        op=ALU.mult,
                    )

        def quantize_lg(k):
            lg_codes[k] = work.tile([P, WORD_PASSES * PAIR_DOCS], U32, name="lg_codes", align_bytes=64)
            lg_scales[k] = work.tile([P, WORD_PASSES * PAIR_DOCS], U8, name="lg_scales", align_bytes=64)
            nc.vector.quantize_mx(out=lg_codes[k][:].bitcast(FP8X4), scales=lg_scales[k][:], in_=lg_packed[k][:])

        def score_passes(out, k, gq, t, lo, width):
            for gw in range(WORD_PASSES):
                first = K_PASS * (WORD_PASSES * gq + gw) + P * t
                q_cols = slice(first, first + P)
                lg_cols = slice(PAIR_DOCS * gw + lo, PAIR_DOCS * gw + lo + width)
                nc.tensor.matmul_mx(
                    out=out,
                    lhsT=q_codes[:, q_cols].bitcast(FP8X4),
                    lhsT_scale=q_scales[:, q_cols],
                    rhs=lg_codes[k][:, lg_cols].bitcast(FP8X4),
                    rhs_scale=lg_scales[k][:, lg_cols],
                    start=(gw == 0),
                    stop=(gw == WORD_PASSES - 1),
                )

        def new_result(k, gq):
            result[k, gq] = work.tile([P, PACK, PAIR_DOCS], F32, name="result", bufs=RESULT_BUFS)
            result_packed[k, gq] = work.tile(
                [P, PAIR_DOCS * PACK], BF16, name="result_packed", bufs=RESULT_PACKED_BUFS, align_bytes=64
            )

        def store_result(k, gq):
            dst = out_0[K_PASS * gq : K_PASS * (gq + 1), pair_docs(k)].rearrange("(p t) m -> p t m", t=PACK)
            nc.sync.dma_start(out=dst, in_=result[k, gq][:])

        def scores_by_slot(k, gq):
            new_result(k, gq)
            for t0 in range(0, PACK, 2):
                bank = psum.tile([P, 2, PAIR_DOCS], F32, name="slot_bank", tag="product")
                for s in range(2):
                    score_passes(bank[:, s, :], k, gq, t0 + s, 0, PAIR_DOCS)
                nc.scalar.copy(out=result[k, gq][:, t0 : t0 + 2, :], in_=bank[:])
            store_result(k, gq)

        def scores_by_tile(k, gq):
            new_result(k, gq)
            banks = []
            for j in range(2):
                banks.append(psum.tile([P, PACK, P], F32, name="tile_bank", tag="product"))
                for t in range(PACK):
                    score_passes(banks[j][:, t, :], k, gq, t, P * j, P)
                nc.scalar.copy(out=result[k, gq][:, :, P * j : P * (j + 1)], in_=banks[j][:])
            store_result(k, gq)
            for j in range(2):
                nc.scalar.copy(
                    out=result_packed[k, gq][:, BANK * j : BANK * (j + 1)].rearrange("p (m t) -> p m t", t=PACK),
                    in_=banks[j][:].rearrange("p t m -> p m t"),
                )

        def pack_result(k, gq):
            nc.vector.tensor_copy(
                out=result_packed[k, gq][:].rearrange("p (c i t) -> p c t i", t=PACK, i=LINE),
                in_=result[k, gq][:].rearrange("p t (c i) -> p c t i", i=LINE),
            )

        def quantize_result(k):
            cols = pair_docs(k)
            result_codes[k] = work.tile([P, QUERY_GROUPS, PAIR_DOCS], U32, name="result_codes", align_bytes=64)
            for gq in range(QUERY_GROUPS):
                if k < EARLY_SCALE_PAIRS:
                    scales = early_scales[:, gq, cols]
                else:
                    scales = late_scales[:, gq, cols.start - early_docs : cols.stop - early_docs]
                nc.vector.quantize_mx(
                    out=result_codes[k][:, gq, :].bitcast(FP8X4), scales=scales, in_=result_packed[k, gq][:]
                )

        def store_codes(k):
            dst = out_1[:, :, pair_docs(k), :].rearrange("g p m t -> p g (m t)").bitcast(I32)
            nc.sync.dma_start(out=dst, in_=result_codes[k][:].bitcast(I32))

        def store_scales(queue, scales, cols):
            for quad in range(SCALE_QUADS):
                dst = out_2[:, 4 * quad : 4 * quad + 4, cols].rearrange("g r m -> r g m").bitcast(I32)
                queue.dma_start(out=dst, in_=scales[32 * quad : 32 * quad + 4, :, :].bitcast(I32))

        nc.vector.memset(w_scales[:].bitcast(I32), 0)
        nc.vector.memset(warm[:], 0.0)
        nc.scalar.dma_start(out=b_cols[:], in_=b.rearrange("(w p t) -> p w t", p=P, t=PACK))
        nc.scalar.activation(out=warm[:], in_=warm[:], func=ACT.Exp)
        make_identity(nc, ident[:])
        load_dv(0)
        nc.sync.dma_start(out=w_codes[:].bitcast(I32), in_=wv_words[0].bitcast(I32))
        for quad in range(SCALE_QUADS):
            nc.sync.dma_start(
                out=w_scales[32 * quad : 32 * quad + 4, :].bitcast(I32),
                in_=wv_scales[0, 4 * quad : 4 * quad + 4, :].bitcast(I32),
            )
        load_dv(1)
        load_f(0)
        load_dv(2)
        load_f(1)
        load_dv(3)
        nc.sync.dma_start(out=c_cols[:], in_=c.rearrange("(w p t) -> p w t", p=P, t=PACK))
        nc.sync.dma_start(out=g_cols[:], in_=g.rearrange("(w p t) -> p w t", p=P, t=PACK))
        q_load_after = (3, 5)
        for k in range(2, PAIRS):
            load_f(k)
            if k + 2 < PAIRS:
                load_dv(k + 2)
            if k in q_load_after:
                load_q(q_load_after.index(k))

        nc.vector.memset(shift_cols[:], 0.0)
        nc.vector.tensor_tensor(
            out=selector[:],
            in0=ident[:, 0:PACK].unsqueeze(2).to_broadcast([P, PACK, P]),
            in1=ident[:, PACK : PACK + 1].unsqueeze(2).to_broadcast([P, PACK, P]),
            op=ALU.add,
        )
        nc.vector.tensor_copy(out=b_cols_f32[:], in_=b_cols[:])
        transpose_dv(0)
        copy_dv(0)
        quantize_dv(0)
        for gw in range(WORD_PASSES):
            b_bank = psum.tile([P, PACK, P], F32, name="b_bank", tag="turn")
            for t in range(PACK):
                nc.tensor.transpose(b_bank[:, t, :], b_cols_f32[:, gw, t : t + 1].to_broadcast([P, P]), ident[:])
            nc.scalar.copy(out=pass_of(b_rows[:], gw), in_=b_bank[:])
        logits(0)
        transpose_dv(1)
        logits(1)
        sum_f(0)
        copy_dv(1)
        add_bias(0)
        sum_f(1)
        row_max(0)
        exponentiate(0)
        quantize_dv(1)

        for i in range(1, TILES + 1):
            h = i - FIRST_Q_STEP
            if i < TILES:
                add_bias(i)
            if i + 1 < TILES:
                if i % 2 == 0 and i // 2 + 1 < PAIRS:
                    quantize_dv(i // 2 + 1)
                logits(i + 1)
            if i == 1:
                transpose_dv(2)
                copy_dv(2)
            if i % 2 == 1 and (i + 5) // 2 < PAIRS:
                transpose_dv((i + 5) // 2)
            if 0 <= h < Q_HALVES:
                transpose_q(h)
            if i % 2 == 0 and (i + 4) // 2 < PAIRS:
                copy_dv((i + 4) // 2)
            if 0 <= h - 1 < Q_HALVES:
                copy_q(h - 1)
            if i + 1 < TILES - TENSOR_F_SUMS:
                sum_f(i + 1)
            if i >= 2:
                row_max(i - 1)
                exponentiate(i - 1)
            if h % 2 == 0 and 0 <= h // 2 - 2 < EARLY_Q_UNITS:
                quantize_q(h // 2 - 2)
            if i in c_chain:
                c_chain[i]()
            if i == TILES - 3:
                invert_sums(0, EARLY_STATS)
            if i == TILES - 2:
                ratio(0, EARLY_STATS)
                make_ln_scale(0, EARLY_STATS)

        mix(0)
        logarithm(0)
        lay_shift(0)
        for i in range(1, MIX_LEAD):
            mix(i)
            if i == WARM_AFTER_MIX:
                nc.vector.tensor_copy(out=ident_bf16[:], in_=ident[:])
                sum_f_on_tensor()
        for unit in range(EARLY_Q_UNITS, Q_UNITS):
            quantize_q(unit)
        nc.vector.tensor_reduce(
            out=f_sum[:, TILES - TENSOR_F_SUMS : TILES], in_=small_bank["f"][:], axis=AX.X, op=ALU.add
        )
        for i in range(1, LOG_LEAD):
            logarithm(i)
        transpose_log(0)

        def scalar_packs(k, gq):
            return k < SCALAR_PACKS_BOTH or (k < SCALAR_PACKS_ONE and gq == 1)

        for k in range(PAIRS + 2):
            if k < PAIRS:
                apply_gain(k)
            if k == 1:
                ratio(EARLY_STATS, TILES)
                make_ln_scale(EARLY_STATS, TILES)
            if 2 * k + MIX_LEAD < TILES:
                mix(2 * k + MIX_LEAD)
            if k < PAIRS:
                quantize_lg(k)
            if 0 <= k - 2:
                quantize_result(k - 2)
            if k == 0:
                invert_sums(EARLY_STATS, TILES)
            if 2 * k + 1 + MIX_LEAD < TILES:
                mix(2 * k + 1 + MIX_LEAD)
            if 0 <= k - 1 < PAIRS:
                for gq in range(QUERY_GROUPS):
                    if scalar_packs(k - 1, gq):
                        scores_by_tile(k - 1, gq)
                    else:
                        scores_by_slot(k - 1, gq)
            if 0 <= k - 2:
                store_codes(k - 2)
            if k - 2 == EARLY_SCALE_PAIRS - 1:
                store_scales(nc.sync, early_scales, slice(0, early_docs))
            for i in (2 * k + LOG_LEAD, 2 * k + 1 + LOG_LEAD):
                if i < TILES:
                    logarithm(i)
            if k + 1 < PAIRS:
                lay_shift(k + 1)
                transpose_log(k + 1)
            if 0 <= k - 1 < PAIRS:
                for gq in range(QUERY_GROUPS):
                    if not scalar_packs(k - 1, gq):
                        pack_result(k - 1, gq)
        store_scales(nc.scalar, late_scales, slice(early_docs, N_DOCS))
